import numpy as np
import ml_dtypes


def mxq(x, axis, fmt="e4m3"):
    dtype, down = {"e4m3": (ml_dtypes.float8_e4m3fn, 7), "e5m2": (ml_dtypes.float8_e5m2, 14)}[fmt]
    v = np.moveaxis(np.asarray(x, np.float32).astype(ml_dtypes.bfloat16).astype(np.float64), axis, -1)
    blocks = v.reshape(v.shape[:-1] + (-1, 32))
    amax = np.abs(blocks).max(-1, keepdims=True)
    byte = np.maximum(np.where(amax > 0, np.frexp(amax)[1] - 1 + 127, 0) - down, 1)
    scale = np.exp2(byte - 127.0)
    codes = (blocks / scale).astype(np.float32).astype(dtype).astype(np.float64)
    return np.moveaxis((codes * scale).reshape(v.shape), -1, axis)


WIDE = False


def mx_kscale(k):
    if not WIDE:
        return np.ones(k)
    levels = np.array([10, -10, 5, -5, 0])
    if k % 512:
        return np.exp2(np.random.permutation(np.resize(levels, k // 32))).repeat(32)
    a = np.empty((k // 512, 16))
    for p in range(k // 512):
        a[p, :8] = np.random.permutation(np.resize(levels, 8))
        for g in range(8):
            far = levels[np.abs(levels - a[p, g]) >= 10]
            a[p, g + 8] = far[np.random.randint(len(far))]
    return np.exp2(a.ravel()).repeat(32)


def f64(x):
    return np.asarray(x).astype(np.float64)


def striped8(idx):
    return np.concatenate([x.reshape(-1, 16).T for x in idx]).astype(np.uint16)


def runs(offs, k):
    lists = np.stack([offs[16 * r : 16 * r + 16].T.reshape(-1) for r in range(8)]).astype(np.int64)
    return lists[np.arange(k) % 512 // 64]


def pack_weight(w):
    k, n = w.shape
    w = f64(np.asarray(w, np.float32).astype(ml_dtypes.bfloat16)).reshape(k // 32, 32, n)
    amax = np.abs(w).max(1)
    byte = np.clip(np.where(amax > 0, np.frexp(amax)[1] - 1 + 127 - 7, 1), 1, 254)
    scaled = (w * np.exp2(127.0 - byte)[:, None, :]).reshape(k, n).astype(np.float32)
    words = np.ascontiguousarray(scaled.reshape(k // 512, 128, 4, n).transpose(0, 1, 3, 2)).astype(ml_dtypes.float8_e4m3fn).view(np.uint8)
    return words, np.ascontiguousarray(byte.astype(np.uint8).reshape(k // 512, 16, n))


def unpack_weight(words, scales):
    g, p, n, _ = words.shape
    vals = np.ascontiguousarray(words).view(ml_dtypes.float8_e4m3fn).astype(np.float64) * np.repeat(np.exp2(scales.astype(np.float64) - 127.0), 8, axis=1)[..., None]
    return vals.transpose(0, 1, 3, 2).reshape(g * 512, n)


E2M1 = np.array([0.0, 0.5, 1.0, 1.5, 2.0, 3.0, 4.0, 6.0, -0.0, -0.5, -1.0, -1.5, -2.0, -3.0, -4.0, -6.0])


def pack_fp4(w):
    k, n = w.shape
    w = f64(np.asarray(w, np.float32).astype(ml_dtypes.bfloat16)).reshape(k // 32, 32, n)
    amax = np.abs(w).max(1)
    mant, ex = np.frexp(amax / 6.0)
    byte = np.clip(np.where(amax > 0, np.where(mant > 0.5, ex, ex - 1) + 127, 1), 1, 254)
    scaled = (w * np.exp2(127.0 - byte)[:, None, :]).reshape(k, n).astype(np.float32)
    c = np.ascontiguousarray(scaled.reshape(k // 512, 128, 4, n).transpose(0, 1, 3, 2)).astype(ml_dtypes.float4_e2m1fn).view(np.uint8) & 0xF
    words = (c[..., 0::2] | (c[..., 1::2] << 4)).reshape(k // 512, 128, 2 * n)
    return np.ascontiguousarray(words), np.ascontiguousarray(byte.astype(np.uint8).reshape(k // 512, 16, n))


def unpack_fp4(words, scales):
    g, _, n = scales.shape
    words = np.ascontiguousarray(words).reshape(g, 128, n, 2)
    nib = np.empty((g, 128, n, 4), np.uint8)
    nib[..., 0::2] = words & 0xF
    nib[..., 1::2] = words >> 4
    vals = E2M1[nib] * np.repeat(np.exp2(scales.astype(np.float64) - 127.0), 8, axis=1)[..., None]
    return vals.transpose(0, 1, 3, 2).reshape(g * 512, n)


def relu(v):
    return np.maximum(v, 0.0)

def planes(y):
    n, m = y.shape
    v = y.astype(np.float32).astype(ml_dtypes.bfloat16).astype(np.float64).reshape(n // 32, 32, m)
    top = np.abs(v).max(1)
    byte = np.clip(np.where(top > 0, np.frexp(top)[1] - 1 + 127 - 7, 1), 1, 254)
    codes = (v * np.exp2(127.0 - byte)[:, None, :]).reshape(n, m).astype(np.float32).astype(ml_dtypes.float8_e4m3fn).view(np.uint8)
    words = codes.reshape(n // 512, 128, 4, m).transpose(0, 1, 3, 2)
    return np.ascontiguousarray(words), np.ascontiguousarray(byte.astype(np.uint8).reshape(n // 512, 16, m))


K, T, S, V, N, H = 512, 2048, 512, 256, 512, 512


def setup_inputs():
    n = np.random.standard_normal
    s = mx_kscale(K)[:, None]
    u = mx_kscale(H)
    packed_xT = pack_weight(n((K, T)) * s)
    packed_w2 = pack_fp4(n((H, N)) / np.sqrt(H) / u[:, None])
    perm = np.stack([np.random.permutation(S) for _ in range(8)])
    return {
        "x_words": packed_xT[0],
        "x_scales": packed_xT[1],
        "w1": (n((K, H)) / np.sqrt(K) / s * u).astype(np.float32),
        "w2_words": packed_w2[0],
        "w2_scales": packed_w2[1],
        "offs": striped8(np.stack([np.random.permutation(T)[:S] for _ in range(8)])),
        "la": striped8(perm[:, :V]),
        "lb": striped8(perm[:, V:]),
    }


def reference(x_words, x_scales, w1, w2_words, w2_scales, offs, la, lb):
    xq = unpack_weight(x_words, x_scales)[np.arange(K)[:, None], runs(offs, K)]
    y = mxq(f64(w1), 0, "e4m3").T @ xq
    a = y[np.arange(H)[:, None], runs(la, H)]
    b = y[np.arange(H)[:, None], runs(lb, H)]
    mx = np.maximum(a, b)
    mn = np.minimum(a, b)
    p = np.zeros((H, S))
    p[np.arange(H)[:, None], runs(la, H)] = mn
    zs = p.copy()
    zs[np.arange(H)[:, None], runs(lb, H)] = mx
    z = relu(zs)
    out_0 = unpack_fp4(w2_words, w2_scales).T @ mxq(z, 0, "e4m3")
    return (out_0,) + planes(out_0)

@@ -1,0 +1,251 @@
+from contextlib import ExitStack
+
+import concourse.mybir as mybir
+
+K, T, S, V, N, H = 512, 2048, 512, 256, 512, 512
+FLOPS = 2 * K * H * S + 2 * H * N * S
+
+F32 = mybir.dt.float32
+BF16 = mybir.dt.bfloat16
+I32 = mybir.dt.int32
+U32 = mybir.dt.uint32
+U16 = mybir.dt.uint16
+U8 = mybir.dt.uint8
+FP8X4 = mybir.dt.float8_e4m3fn_x4
+FP4X4 = mybir.dt.float4_e2m1fn_x4
+ALU = mybir.AluOpType
+RELU = mybir.ActivationFunctionType.Relu
+
+P = 128
+PACK = 4
+QUADS = 4
+HALF = S // 2
+CHUNK = 128
+CHUNKS = S // CHUNK
+M_SCALAR = 48
+
+
+def tile_picked_sortpair_relu_po_kernel(
+    tc, x_words, x_scales, w1, w2_words, w2_scales, offs, la, lb, out_0, out_1, out_2
+):
+    nc = tc.nc
+    with ExitStack() as ctx:
+        keep = ctx.enter_context(tc.tile_pool(name="keep", bufs=1))
+        psum = ctx.enter_context(tc.psum_pool(name="psum", bufs=8))
+
+        def tile(shape, dtype, name):
+            return keep.tile(shape, dtype, name=name, align_bytes=64)
+
+        offs_sb = tile([P, S // 16], U16, "offs_sb")
+        la_sb = tile([P, V // 16], U16, "la_sb")
+        lb_sb = tile([P, V // 16], U16, "lb_sb")
+        xs_table = tile([P, T], U8, "xs_table")
+        xs_picked = tile([P, S], U8, "xs_picked")
+        xs_plane = tile([P, S], U8, "xs_plane")
+        xw_table = tile([P, T], U32, "xw_table")
+        xw_picked = tile([P, S], U32, "xw_picked")
+        w1_raw = tile([P, PACK, H], F32, "w1_raw")
+        w1_bf = tile([P, PACK * H], BF16, "w1_bf")
+        w1_codes = tile([P, H], U32, "w1_codes")
+        w1_plane = tile([P, H], U8, "w1_plane")
+        w2w_raw = tile([P, 2 * N], U8, "w2w_raw")
+        w2s_raw = tile([P, N], U8, "w2s_raw")
+        w2_codes = tile([P, 2 * N], U8, "w2_codes")
+        w2_plane = tile([P, N], U8, "w2_plane")
+        warm_in = tile([P, 1], F32, "warm_in")
+        warm_out = tile([P, 1], F32, "warm_out")
+
+        nc.vector.memset(xs_table[:].bitcast(I32), 0)
+        nc.vector.memset(warm_in[:], 0.0)
+        nc.vector.memset(xs_plane[:].bitcast(I32), 0)
+        nc.gpsimd.memset(w2s_raw[:].bitcast(I32), 0)
+
+        nc.sync.dma_start(offs_sb[:], offs)
+        nc.scalar.dma_start(out=xs_table[0:P:8, :].bitcast(I32), in_=x_scales[0].bitcast(I32))
+        nc.scalar.activation(out=warm_out[:], in_=warm_in[:], func=RELU)
+        nc.sync.dma_start(la_sb[:], la)
+        nc.sync.dma_start(lb_sb[:], lb)
+        nc.sync.dma_start(out=w1_raw[:], in_=w1.rearrange("(p j) c -> p j c", j=PACK))
+        nc.sync.dma_start(
+            out=xw_table[:].bitcast(I32), in_=x_words[0].rearrange("p c r -> p (c r)").bitcast(I32)
+        )
+        nc.sync.dma_start(out=w2w_raw[:].bitcast(I32), in_=w2_words[0].bitcast(I32))
+        for q in range(QUADS):
+            nc.gpsimd.dma_start(
+                out=w2s_raw[32 * q : 32 * q + 4, :].bitcast(I32), in_=w2_scales[0][4 * q : 4 * q + 4, :].bitcast(I32)
+            )
+
+        nc.vector.tensor_copy(xs_picked[:], xs_table[:].indirect(offs_sb[:]))
+        for q in range(QUADS):
+            nc.scalar.dma_start(
+                out=xs_plane[32 * q : 32 * q + 4, :].bitcast(I32),
+                in_=xs_picked[32 * q : 32 * q + 32 : 8, :].bitcast(I32),
+            )
+
+        w1_dst = w1_bf[:].rearrange("p (t m j) -> p m j t", t=PACK, j=PACK)
+        w1_src = w1_raw[:].rearrange("p j (m t) -> p m j t", t=PACK)
+        nc.scalar.copy(out=w1_dst[:, :M_SCALAR], in_=w1_src[:, :M_SCALAR])
+        nc.vector.tensor_copy(out=w1_dst[:, M_SCALAR:], in_=w1_src[:, M_SCALAR:])
+        nc.vector.quantize_mx(out=w1_codes[:].bitcast(FP8X4), scales=w1_plane[:], in_=w1_bf[:])
+
+        y = [tile([P, S], F32, "y%d" % t) for t in range(PACK)]
+
+        def first_product(t, cols):
+            width = cols.stop - cols.start
+            bank = psum.tile([P, S], F32, name="bank")
+            rows = slice(P * t, P * (t + 1))
+            nc.tensor.matmul_mx(
+                out=bank[:, :width],
+                lhsT=w1_codes[:, rows].bitcast(FP8X4),
+                lhsT_scale=w1_plane[:, rows],
+                rhs=xw_picked[:, cols].bitcast(FP8X4),
+                rhs_scale=xs_plane[:, cols],
+                start=True,
+                stop=True,
+            )
+            nc.scalar.activation(out=y[t][:, cols], in_=bank[:, :width], func=RELU)
+
+        for h in range(2):
+            cols = slice(HALF * h, HALF * (h + 1))
+            nc.vector.tensor_copy(
+                xw_picked[:, cols], xw_table[:].indirect(offs_sb[:, HALF // 16 * h : HALF // 16 * (h + 1)])
+            )
+            first_product(0, cols)
+        for t in range(1, PACK):
+            first_product(t, slice(0, S))
+
+        nc.vector.tensor_copy(
+            out=w2_codes[:].rearrange("p (t m b) -> p m t b", t=PACK, b=2),
+            in_=w2w_raw[:].rearrange("p (m t b) -> p m t b", t=PACK, b=2),
+        )
+        nc.vector.tensor_copy(
+            out=w2_plane[:].rearrange("p (t m) -> p m t", t=PACK),
+            in_=w2s_raw[:].rearrange("p (m t) -> p m t", t=PACK),
+        )
+
+        a = [tile([P, V], F32, "a%d" % t) for t in range(PACK)]
+        b = [tile([P, V], F32, "b%d" % t) for t in range(PACK)]
+        mn = [tile([P, V], F32, "mn%d" % t) for t in range(PACK)]
+        mx = [tile([P, V], F32, "mx%d" % t) for t in range(PACK)]
+        z = [tile([P, S], F32, "z%d" % t) for t in range(PACK)]
+        z_bf = tile([P, S, PACK], BF16, "z_bf")
+
+        def fetch_a(t):
+            nc.vector.tensor_copy(a[t][:], y[t][:].indirect(la_sb[:]))
+
+        def fetch_b(t):
+            nc.vector.tensor_copy(b[t][:], y[t][:].indirect(lb_sb[:]))
+
+        def compare(t):
+            nc.vector.tensor_tensor(mn[t][:], a[t][:], b[t][:], ALU.min)
+            nc.vector.tensor_tensor(mx[t][:], a[t][:], b[t][:], ALU.max)
+
+        def put_a(t):
+            nc.vector.tensor_copy(z[t][:].indirect(la_sb[:]), mn[t][:])
+
+        def put_b(t):
+            nc.vector.tensor_copy(z[t][:].indirect(lb_sb[:]), mx[t][:])
+
+        fetch_a(0)
+        fetch_b(0)
+        fetch_a(1)
+        compare(0)
+        fetch_b(1)
+        put_a(0)
+        compare(1)
+        put_b(0)
+        nc.scalar.copy(out=z_bf[:, :, 0], in_=z[0][:])
+        fetch_a(2)
+        put_a(1)
+        fetch_b(2)
+        put_b(1)
+        nc.scalar.copy(out=z_bf[:, :, 1], in_=z[1][:])
+        fetch_a(3)
+        compare(2)
+        fetch_b(3)
+        put_a(2)
+        compare(3)
+        put_b(2)
+        nc.scalar.copy(out=z_bf[:, :, 2:4], in_=z[2][:].unsqueeze(2).to_broadcast([P, S, 2]))
+        put_a(3)
+        put_b(3)
+
+        z_codes = tile([P, S], U32, "z_codes")
+        z_plane = tile([P, S], U8, "z_plane")
+        o_codes = tile([P, S], U32, "o_codes")
+        o_plane = tile([P, S], U8, "o_plane")
+        out_rows = out_0.rearrange("(p t) c -> p t c", t=PACK)
+        words_dst = out_1[0].rearrange("p c r -> p (c r)").bitcast(I32)
+        chunk = [slice(CHUNK * c, CHUNK * (c + 1)) for c in range(CHUNKS)]
+        banks = {}
+        o_f32 = [tile([P, PACK, CHUNK], F32, "o_f32_%d" % c) for c in range(CHUNKS)]
+        o_bf = [tile([P, CHUNK, PACK], BF16, "o_bf_%d" % c) for c in range(CHUNKS)]
+
+        def finish_z(c):
+            nc.vector.tensor_copy(out=z_bf[:, chunk[c], 3], in_=z[3][:, chunk[c]])
+
+        def second_product(c):
+            nc.vector.quantize_mx(
+                out=z_codes[:, chunk[c]].bitcast(FP8X4),
+                scales=z_plane[:, chunk[c]],
+                in_=z_bf[:, chunk[c], :].rearrange("p c t -> p (c t)"),
+            )
+            bank = psum.tile([P, S], F32, name="bank")
+            banks[c] = bank
+            for t in range(PACK):
+                nc.tensor.matmul_mx(
+                    out=bank[:, CHUNK * t : CHUNK * (t + 1)],
+                    lhsT=w2_codes[:, 2 * P * t : 2 * P * (t + 1)].bitcast(FP4X4),
+                    lhsT_scale=w2_plane[:, P * t : P * (t + 1)],
+                    rhs=z_codes[:, chunk[c]].bitcast(FP8X4),
+                    rhs_scale=z_plane[:, chunk[c]],
+                    start=True,
+                    stop=True,
+                )
+
+        def leave_f32(c):
+            nc.scalar.copy(out=o_f32[c][:].rearrange("p t c -> p (t c)"), in_=banks[c][:])
+            nc.sync.dma_start(out=out_rows[:, :, chunk[c]], in_=o_f32[c][:])
+
+        def weave_from_sbuf(c):
+            nc.vector.tensor_copy(
+                out=o_bf[c][:].rearrange("p (g i) t -> p g t i", i=4),
+                in_=o_f32[c][:].rearrange("p t (g i) -> p g t i", i=4),
+            )
+
+        def weave_from_psum(c):
+            nc.vector.tensor_copy(out=o_bf[c][:], in_=banks[c][:].rearrange("p (t c) -> p c t", t=PACK))
+
+        def leave_codes(c):
+            nc.vector.quantize_mx(
+                out=o_codes[:, chunk[c]].bitcast(FP8X4),
+                scales=o_plane[:, chunk[c]],
+                in_=o_bf[c][:].rearrange("p c t -> p (c t)"),
+            )
+            nc.sync.dma_start(out=words_dst[:, chunk[c]], in_=o_codes[:, chunk[c]].bitcast(I32))
+
+        finish_z(0)
+        finish_z(1)
+        second_product(0)
+        finish_z(2)
+        second_product(1)
+        finish_z(3)
+        second_product(2)
+        second_product(3)
+        leave_f32(0)
+        weave_from_sbuf(0)
+        leave_f32(1)
+        weave_from_sbuf(1)
+        leave_codes(0)
+        leave_f32(2)
+        weave_from_sbuf(2)
+        leave_codes(1)
+        weave_from_psum(3)
+        leave_f32(3)
+        leave_codes(2)
+        leave_codes(3)
+        for q in range(QUADS):
+            queue = nc.scalar if q % 2 else nc.sync
+            queue.dma_start(
+                out=out_2[0][4 * q : 4 * q + 4, :].bitcast(I32), in_=o_plane[32 * q : 32 * q + 4, :].bitcast(I32)
+            )

@@ -22,7 +22,7 @@ QUADS = 4
 HALF = S // 2
 CHUNK = 128
 CHUNKS = S // CHUNK
-M_SCALAR = 48
+M_SCALAR = 44
 
 
 def tile_picked_sortpair_relu_po_kernel(
@@ -33,8 +33,13 @@ def tile_picked_sortpair_relu_po_kernel(
         keep = ctx.enter_context(tc.tile_pool(name="keep", bufs=1))
         psum = ctx.enter_context(tc.psum_pool(name="psum", bufs=8))
 
+        shared = ctx.enter_context(tc.tile_pool(name="shared", bufs=1))
+
         def tile(shape, dtype, name):
             return keep.tile(shape, dtype, name=name, align_bytes=64)
+
+        def tile_at(offset, shape, dtype, name):
+            return shared.tile(shape, dtype, name=name, align_bytes=64, offset=offset)
 
         offs_sb = tile([P, S // 16], U16, "offs_sb")
         la_sb = tile([P, V // 16], U16, "la_sb")
@@ -42,7 +47,7 @@ def tile_picked_sortpair_relu_po_kernel(
         xs_table = tile([P, T], U8, "xs_table")
         xs_picked = tile([P, S], U8, "xs_picked")
         xs_plane = tile([P, S], U8, "xs_plane")
-        xw_table = tile([P, T], U32, "xw_table")
+        xw_table = tile_at(0, [P, T], U32, "xw_table")
         xw_picked = tile([P, S], U32, "xw_picked")
         w1_raw = tile([P, PACK, H], F32, "w1_raw")
         w1_bf = tile([P, PACK * H], BF16, "w1_bf")
@@ -50,25 +55,27 @@ def tile_picked_sortpair_relu_po_kernel(
         w1_plane = tile([P, H], U8, "w1_plane")
         w2w_raw = tile([P, 2 * N], U8, "w2w_raw")
         w2s_raw = tile([P, N], U8, "w2s_raw")
-        w2_codes = tile([P, 2 * N], U8, "w2_codes")
-        w2_plane = tile([P, N], U8, "w2_plane")
+        w2_codes = tile_at(0, [P, 2 * N], U8, "w2_codes")
+        w2_plane = tile_at(2 * N, [P, N], U8, "w2_plane")
         warm_in = tile([P, 1], F32, "warm_in")
         warm_out = tile([P, 1], F32, "warm_out")
 
-        nc.vector.memset(xs_table[:].bitcast(I32), 0)
         nc.vector.memset(warm_in[:], 0.0)
         nc.vector.memset(xs_plane[:].bitcast(I32), 0)
         nc.gpsimd.memset(w2s_raw[:].bitcast(I32), 0)
 
         nc.sync.dma_start(offs_sb[:], offs)
-        nc.scalar.dma_start(out=xs_table[0:P:8, :].bitcast(I32), in_=x_scales[0].bitcast(I32))
+        nc.scalar.dma_start(
+            out=xs_table[:].bitcast(I32),
+            in_=x_scales[0].bitcast(I32).unsqueeze(1).to_broadcast([16, 8, T // 4]),
+        )
         nc.scalar.activation(out=warm_out[:], in_=warm_in[:], func=RELU)
         nc.sync.dma_start(la_sb[:], la)
-        nc.sync.dma_start(lb_sb[:], lb)
         nc.sync.dma_start(out=w1_raw[:], in_=w1.rearrange("(p j) c -> p j c", j=PACK))
         nc.sync.dma_start(
             out=xw_table[:].bitcast(I32), in_=x_words[0].rearrange("p c r -> p (c r)").bitcast(I32)
         )
+        nc.sync.dma_start(lb_sb[:], lb)
         nc.sync.dma_start(out=w2w_raw[:].bitcast(I32), in_=w2_words[0].bitcast(I32))
         for q in range(QUADS):
             nc.gpsimd.dma_start(
@@ -165,9 +172,13 @@ def tile_picked_sortpair_relu_po_kernel(
         fetch_b(3)
         put_a(2)
         compare(3)
-        put_b(2)
-        nc.scalar.copy(out=z_bf[:, :, 2:4], in_=z[2][:].unsqueeze(2).to_broadcast([P, S, 2]))
         put_a(3)
+        put_b(2)
+        chunk = [slice(CHUNK * c, CHUNK * (c + 1)) for c in range(CHUNKS)]
+        for c in range(CHUNKS):
+            nc.scalar.copy(
+                out=z_bf[:, chunk[c], 2:4], in_=z[2][:, chunk[c]].unsqueeze(2).to_broadcast([P, CHUNK, 2])
+            )
         put_b(3)
 
         z_codes = tile([P, S], U32, "z_codes")
@@ -176,13 +187,13 @@ def tile_picked_sortpair_relu_po_kernel(
         o_plane = tile([P, S], U8, "o_plane")
         out_rows = out_0.rearrange("(p t) c -> p t c", t=PACK)
         words_dst = out_1[0].rearrange("p c r -> p (c r)").bitcast(I32)
-        chunk = [slice(CHUNK * c, CHUNK * (c + 1)) for c in range(CHUNKS)]
         banks = {}
         o_f32 = [tile([P, PACK, CHUNK], F32, "o_f32_%d" % c) for c in range(CHUNKS)]
         o_bf = [tile([P, CHUNK, PACK], BF16, "o_bf_%d" % c) for c in range(CHUNKS)]
 
         def finish_z(c):
-            nc.vector.tensor_copy(out=z_bf[:, chunk[c], 3], in_=z[3][:, chunk[c]])
+            copy = nc.scalar.copy if c % 2 else nc.vector.tensor_copy
+            copy(out=z_bf[:, chunk[c], 3], in_=z[3][:, chunk[c]])
 
         def second_product(c):
             nc.vector.quantize_mx(
@@ -190,11 +201,12 @@ def tile_picked_sortpair_relu_po_kernel(
                 scales=z_plane[:, chunk[c]],
                 in_=z_bf[:, chunk[c], :].rearrange("p c t -> p (c t)"),
             )
-            bank = psum.tile([P, S], F32, name="bank")
-            banks[c] = bank
+            per_bank = 2 if c == 0 else PACK
+            banks[c] = [psum.tile([P, S], F32, name="bank") for u in range(PACK // per_bank)]
             for t in range(PACK):
+                slot = t % per_bank
                 nc.tensor.matmul_mx(
-                    out=bank[:, CHUNK * t : CHUNK * (t + 1)],
+                    out=banks[c][t // per_bank][:, CHUNK * slot : CHUNK * (slot + 1)],
                     lhsT=w2_codes[:, 2 * P * t : 2 * P * (t + 1)].bitcast(FP4X4),
                     lhsT_scale=w2_plane[:, P * t : P * (t + 1)],
                     rhs=z_codes[:, chunk[c]].bitcast(FP8X4),
@@ -204,8 +216,14 @@ def tile_picked_sortpair_relu_po_kernel(
                 )
 
         def leave_f32(c):
-            nc.scalar.copy(out=o_f32[c][:].rearrange("p t c -> p (t c)"), in_=banks[c][:])
+            nc.scalar.copy(out=o_f32[c][:].rearrange("p t c -> p (t c)"), in_=banks[c][0][:])
             nc.sync.dma_start(out=out_rows[:, :, chunk[c]], in_=o_f32[c][:])
+
+        def leave_f32_halves(c):
+            for u, copy in enumerate((nc.scalar.copy, nc.vector.tensor_copy)):
+                rows = slice(2 * u, 2 * u + 2)
+                copy(out=o_f32[c][:, rows, :].rearrange("p t c -> p (t c)"), in_=banks[c][u][:, : 2 * CHUNK])
+                nc.sync.dma_start(out=out_rows[:, rows, chunk[c]], in_=o_f32[c][:, rows, :])
 
         def weave_from_sbuf(c):
             nc.vector.tensor_copy(
@@ -214,7 +232,7 @@ def tile_picked_sortpair_relu_po_kernel(
             )
 
         def weave_from_psum(c):
-            nc.vector.tensor_copy(out=o_bf[c][:], in_=banks[c][:].rearrange("p (t c) -> p c t", t=PACK))
+            nc.vector.tensor_copy(out=o_bf[c][:], in_=banks[c][0][:].rearrange("p (t c) -> p c t", t=PACK))
 
         def leave_codes(c):
             nc.vector.quantize_mx(
@@ -222,17 +240,15 @@ def tile_picked_sortpair_relu_po_kernel(
                 scales=o_plane[:, chunk[c]],
                 in_=o_bf[c][:].rearrange("p c t -> p (c t)"),
             )
-            nc.sync.dma_start(out=words_dst[:, chunk[c]], in_=o_codes[:, chunk[c]].bitcast(I32))
+            if c % 2:
+                cols = slice(chunk[c - 1].start, chunk[c].stop)
+                nc.sync.dma_start(out=words_dst[:, cols], in_=o_codes[:, cols].bitcast(I32))
 
-        finish_z(0)
-        finish_z(1)
-        second_product(0)
-        finish_z(2)
-        second_product(1)
-        finish_z(3)
-        second_product(2)
-        second_product(3)
-        leave_f32(0)
+        for c in range(CHUNKS):
+            finish_z(c)
+        for c in range(CHUNKS):
+            second_product(c)
+        leave_f32_halves(0)
         weave_from_sbuf(0)
         leave_f32(1)
         weave_from_sbuf(1)

@@ -122,12 +122,12 @@ def tile_picked_sortpair_relu_po_kernel(
             first_product(t, slice(0, S))
 
         nc.vector.tensor_copy(
-            out=w2_codes[:].rearrange("p (t m b) -> p m t b", t=PACK, b=2),
-            in_=w2w_raw[:].rearrange("p (m t b) -> p m t b", t=PACK, b=2),
+            out=w2_codes[:].rearrange("p (t m b) -> p t m b", t=PACK, b=2),
+            in_=w2w_raw[:].rearrange("p (m t b) -> p t m b", t=PACK, b=2),
         )
         nc.vector.tensor_copy(
-            out=w2_plane[:].rearrange("p (t m) -> p m t", t=PACK),
-            in_=w2s_raw[:].rearrange("p (m t) -> p m t", t=PACK),
+            out=w2_plane[:].rearrange("p (t m) -> p t m", t=PACK),
+            in_=w2s_raw[:].rearrange("p (m t) -> p t m", t=PACK),
         )
 
         a = [tile([P, V], F32, "a%d" % t) for t in range(PACK)]
@@ -145,13 +145,13 @@ def tile_picked_sortpair_relu_po_kernel(
 
         def compare(t):
             nc.vector.tensor_tensor(mn[t][:], a[t][:], b[t][:], ALU.min)
-            nc.vector.tensor_tensor(mx[t][:], a[t][:], b[t][:], ALU.max)
+            nc.gpsimd.tensor_tensor(mx[t][:], a[t][:], mn[t][:], ALU.subtract)
 
         def put_a(t):
             nc.vector.tensor_copy(z[t][:].indirect(la_sb[:]), mn[t][:])
 
         def put_b(t):
-            nc.vector.tensor_copy(z[t][:].indirect(lb_sb[:]), mx[t][:])
+            nc.vector.tensor_tensor(z[t][:].indirect(lb_sb[:]), b[t][:], mx[t][:], ALU.add)
 
         fetch_a(0)
         fetch_b(0)
@@ -160,18 +160,18 @@ def tile_picked_sortpair_relu_po_kernel(
         fetch_b(1)
         put_a(0)
         compare(1)
+        fetch_a(2)
+        fetch_b(2)
         put_b(0)
         nc.scalar.copy(out=z_bf[:, :, 0], in_=z[0][:])
-        fetch_a(2)
         put_a(1)
-        fetch_b(2)
+        compare(2)
+        fetch_a(3)
+        fetch_b(3)
         put_b(1)
         nc.scalar.copy(out=z_bf[:, :, 1], in_=z[1][:])
-        fetch_a(3)
-        compare(2)
-        fetch_b(3)
-        put_a(2)
         compare(3)
+        put_a(2)
         put_a(3)
         put_b(2)
         chunk = [slice(CHUNK * c, CHUNK * (c + 1)) for c in range(CHUNKS)]
@@ -240,9 +240,10 @@ def tile_picked_sortpair_relu_po_kernel(
                 scales=o_plane[:, chunk[c]],
                 in_=o_bf[c][:].rearrange("p c t -> p (c t)"),
             )
-            if c % 2:
-                cols = slice(chunk[c - 1].start, chunk[c].stop)
-                nc.sync.dma_start(out=words_dst[:, cols], in_=o_codes[:, cols].bitcast(I32))
+
+        def store_words(h):
+            cols = slice(HALF * h, HALF * (h + 1))
+            nc.sync.dma_start(out=words_dst[:, cols], in_=o_codes[:, cols].bitcast(I32))
 
         for c in range(CHUNKS):
             finish_z(c)
@@ -251,15 +252,17 @@ def tile_picked_sortpair_relu_po_kernel(
         leave_f32_halves(0)
         weave_from_sbuf(0)
         leave_f32(1)
-        weave_from_sbuf(1)
         leave_codes(0)
+        weave_from_sbuf(1)
         leave_f32(2)
-        weave_from_sbuf(2)
         leave_codes(1)
+        store_words(0)
         weave_from_psum(3)
         leave_f32(3)
-        leave_codes(2)
+        weave_from_sbuf(2)
         leave_codes(3)
+        leave_codes(2)
+        store_words(1)
         for q in range(QUADS):
             queue = nc.scalar if q % 2 else nc.sync
             queue.dma_start(

@@ -15,6 +15,7 @@ FP8X4 = mybir.dt.float8_e4m3fn_x4
 FP4X4 = mybir.dt.float4_e2m1fn_x4
 ALU = mybir.AluOpType
 RELU = mybir.ActivationFunctionType.Relu
+SIGN = mybir.ActivationFunctionType.Sign
 
 P = 128
 PACK = 4
@@ -130,56 +131,83 @@ def tile_picked_sortpair_relu_po_kernel(
             in_=w2s_raw[:].rearrange("p (m t) -> p t m", t=PACK),
         )
 
-        a = [tile([P, V], F32, "a%d" % t) for t in range(PACK)]
-        b = [tile([P, V], F32, "b%d" % t) for t in range(PACK)]
-        mn = [tile([P, V], F32, "mn%d" % t) for t in range(PACK)]
-        mx = [tile([P, V], F32, "mx%d" % t) for t in range(PACK)]
+        early = range(2)
+        late = range(2, PACK)
+        a_early = tile([P, 2, V], F32, "a_early")
+        b_early = tile([P, 2, V], F32, "b_early")
+        mn_early = tile([P, 2, V], F32, "mn_early")
+        up_early = tile([P, 2, V], F32, "up_early")
+        mx_early = tile([P, 2, V], F32, "mx_early")
+        ab = {t: tile([P, 2, V], F32, "ab%d" % t) for t in late}
+        diff = {t: tile([P, V], F32, "diff%d" % t) for t in late}
+        up = {t: tile([P, V], F32, "up%d" % t) for t in late}
+        take = {t: tile([P, 2, V], F32, "take%d" % t) for t in late}
+        parts = {t: tile([P, 2, V], F32, "parts%d" % t) for t in late}
+        mn_late = {t: tile([P, V], F32, "mn%d" % t) for t in late}
+        mx_late = {t: tile([P, V], F32, "mx%d" % t) for t in late}
+        a = [a_early[:, t, :] for t in early] + [ab[t][:, 0, :] for t in late]
+        b = [b_early[:, t, :] for t in early] + [ab[t][:, 1, :] for t in late]
+        mn = [mn_early[:, t, :] for t in early] + [mn_late[t][:] for t in late]
+        mx = [mx_early[:, t, :] for t in early] + [mx_late[t][:] for t in late]
         z = [tile([P, S], F32, "z%d" % t) for t in range(PACK)]
         z_bf = tile([P, S, PACK], BF16, "z_bf")
 
         def fetch_a(t):
-            nc.vector.tensor_copy(a[t][:], y[t][:].indirect(la_sb[:]))
+            nc.vector.tensor_copy(a[t], y[t][:].indirect(la_sb[:]))
 
         def fetch_b(t):
-            nc.vector.tensor_copy(b[t][:], y[t][:].indirect(lb_sb[:]))
+            nc.vector.tensor_copy(b[t], y[t][:].indirect(lb_sb[:]))
 
         def compare(t):
-            nc.vector.tensor_tensor(mn[t][:], a[t][:], b[t][:], ALU.min)
-            nc.gpsimd.tensor_tensor(mx[t][:], a[t][:], mn[t][:], ALU.subtract)
+            nc.gpsimd.tensor_tensor(diff[t][:], a[t], b[t], ALU.subtract)
+            nc.scalar.activation(out=up[t][:], in_=diff[t][:], func=RELU)
+            nc.scalar.activation(out=take[t][:, 1, :], in_=up[t][:], func=SIGN)
+            nc.scalar.activation(out=take[t][:, 0, :], in_=take[t][:, 1, :], func=RELU, scale=-1.0, bias=1.0)
+
+        def larger(t):
+            nc.gpsimd.tensor_tensor(mx[t], b[t], up[t][:], ALU.add)
+
+        def smaller(t):
+            nc.gpsimd.tensor_tensor(parts[t][:], ab[t][:], take[t][:], ALU.mult)
+            nc.gpsimd.tensor_tensor(mn[t], parts[t][:, 0, :], parts[t][:, 1, :], ALU.add)
 
         def put_a(t):
-            nc.vector.tensor_copy(z[t][:].indirect(la_sb[:]), mn[t][:])
+            nc.vector.tensor_copy(z[t][:].indirect(la_sb[:]), mn[t])
 
         def put_b(t):
-            nc.vector.tensor_tensor(z[t][:].indirect(lb_sb[:]), b[t][:], mx[t][:], ALU.add)
+            nc.vector.tensor_copy(z[t][:].indirect(lb_sb[:]), mx[t])
 
         fetch_a(0)
         fetch_b(0)
         fetch_a(1)
-        compare(0)
         fetch_b(1)
-        put_a(0)
-        compare(1)
         fetch_a(2)
+        nc.vector.tensor_tensor(mn_early[:], a_early[:], b_early[:], ALU.min)
+        nc.gpsimd.tensor_tensor(up_early[:], a_early[:], mn_early[:], ALU.subtract)
         fetch_b(2)
-        put_b(0)
-        nc.scalar.copy(out=z_bf[:, :, 0], in_=z[0][:])
-        put_a(1)
-        compare(2)
         fetch_a(3)
         fetch_b(3)
-        put_b(1)
-        nc.scalar.copy(out=z_bf[:, :, 1], in_=z[1][:])
-        compare(3)
+        nc.gpsimd.tensor_tensor(mx_early[:], b_early[:], up_early[:], ALU.add)
+        for t in late:
+            compare(t)
+        for t in early:
+            put_a(t)
+        for t in late:
+            larger(t)
+        for t in early:
+            put_b(t)
+            nc.scalar.copy(out=z_bf[:, :, t], in_=z[t][:])
+        for t in late:
+            put_b(t)
+        for t in late:
+            smaller(t)
         put_a(2)
-        put_a(3)
-        put_b(2)
         chunk = [slice(CHUNK * c, CHUNK * (c + 1)) for c in range(CHUNKS)]
         for c in range(CHUNKS):
             nc.scalar.copy(
                 out=z_bf[:, chunk[c], 2:4], in_=z[2][:, chunk[c]].unsqueeze(2).to_broadcast([P, CHUNK, 2])
             )
-        put_b(3)
+        put_a(3)
 
         z_codes = tile([P, S], U32, "z_codes")
         z_plane = tile([P, S], U8, "z_plane")
@@ -215,9 +243,9 @@ def tile_picked_sortpair_relu_po_kernel(
                     stop=True,
                 )
 
-        def leave_f32(c):
+        def leave_f32(c, queue):
             nc.scalar.copy(out=o_f32[c][:].rearrange("p t c -> p (t c)"), in_=banks[c][0][:])
-            nc.sync.dma_start(out=out_rows[:, :, chunk[c]], in_=o_f32[c][:])
+            queue.dma_start(out=out_rows[:, :, chunk[c]], in_=o_f32[c][:])
 
         def leave_f32_halves(c):
             for u, copy in enumerate((nc.scalar.copy, nc.vector.tensor_copy)):
@@ -232,7 +260,7 @@ def tile_picked_sortpair_relu_po_kernel(
             )
 
         def weave_from_psum(c):
-            nc.vector.tensor_copy(out=o_bf[c][:], in_=banks[c][0][:].rearrange("p (t c) -> p c t", t=PACK))
+            nc.scalar.copy(out=o_bf[c][:], in_=banks[c][0][:].rearrange("p (t c) -> p c t", t=PACK))
 
         def leave_codes(c):
             nc.vector.quantize_mx(
@@ -241,8 +269,7 @@ def tile_picked_sortpair_relu_po_kernel(
                 in_=o_bf[c][:].rearrange("p c t -> p (c t)"),
             )
 
-        def store_words(h):
-            cols = slice(HALF * h, HALF * (h + 1))
+        def store_words(cols):
             nc.sync.dma_start(out=words_dst[:, cols], in_=o_codes[:, cols].bitcast(I32))
 
         for c in range(CHUNKS):
@@ -251,18 +278,18 @@ def tile_picked_sortpair_relu_po_kernel(
             second_product(c)
         leave_f32_halves(0)
         weave_from_sbuf(0)
-        leave_f32(1)
+        leave_f32(1, nc.sync)
         leave_codes(0)
         weave_from_sbuf(1)
-        leave_f32(2)
+        leave_f32(2, nc.sync)
         leave_codes(1)
-        store_words(0)
+        store_words(slice(0, HALF))
         weave_from_psum(3)
-        leave_f32(3)
         weave_from_sbuf(2)
-        leave_codes(3)
+        leave_f32(3, nc.scalar)
         leave_codes(2)
-        store_words(1)
+        leave_codes(3)
+        store_words(slice(HALF, S))
         for q in range(QUADS):
             queue = nc.scalar if q % 2 else nc.sync
             queue.dma_start(

@@ -57,7 +57,7 @@ def tile_picked_sortpair_relu_po_kernel(
         w2w_raw = tile([P, 2 * N], U8, "w2w_raw")
         w2s_raw = tile([P, N], U8, "w2s_raw")
         w2_codes = tile_at(0, [P, 2 * N], U8, "w2_codes")
-        w2_plane = tile_at(2 * N, [P, N], U8, "w2_plane")
+        w2_plane = tile_at(4 * T, [P, N], U8, "w2_plane")
         warm_in = tile([P, 1], F32, "warm_in")
         warm_out = tile([P, 1], F32, "warm_out")
 
@@ -118,7 +118,8 @@ def tile_picked_sortpair_relu_po_kernel(
             nc.vector.tensor_copy(
                 xw_picked[:, cols], xw_table[:].indirect(offs_sb[:, HALF // 16 * h : HALF // 16 * (h + 1)])
             )
-            first_product(0, cols)
+            for piece in ((cols,), (slice(HALF, HALF + CHUNK), slice(HALF + CHUNK, S)))[h]:
+                first_product(0, piece)
         for t in range(1, PACK):
             first_product(t, slice(0, S))
 
@@ -126,23 +127,19 @@ def tile_picked_sortpair_relu_po_kernel(
             out=w2_codes[:].rearrange("p (t m b) -> p t m b", t=PACK, b=2),
             in_=w2w_raw[:].rearrange("p (m t b) -> p t m b", t=PACK, b=2),
         )
-        nc.vector.tensor_copy(
-            out=w2_plane[:].rearrange("p (t m) -> p t m", t=PACK),
-            in_=w2s_raw[:].rearrange("p (m t) -> p t m", t=PACK),
-        )
 
-        early = range(2)
-        late = range(2, PACK)
-        a_early = tile([P, 2, V], F32, "a_early")
-        b_early = tile([P, 2, V], F32, "b_early")
-        mn_early = tile([P, 2, V], F32, "mn_early")
-        up_early = tile([P, 2, V], F32, "up_early")
-        mx_early = tile([P, 2, V], F32, "mx_early")
+        early = range(1)
+        late = range(1, PACK)
+        a_early = tile([P, 1, V], F32, "a_early")
+        b_early = tile([P, 1, V], F32, "b_early")
+        mn_early = tile([P, 1, V], F32, "mn_early")
+        up_early = tile([P, 1, V], F32, "up_early")
+        mx_early = tile([P, 1, V], F32, "mx_early")
         ab = {t: tile([P, 2, V], F32, "ab%d" % t) for t in late}
         diff = {t: tile([P, V], F32, "diff%d" % t) for t in late}
         up = {t: tile([P, V], F32, "up%d" % t) for t in late}
         take = {t: tile([P, 2, V], F32, "take%d" % t) for t in late}
-        parts = {t: tile([P, 2, V], F32, "parts%d" % t) for t in late}
+        parts = {t: tile_at(4 * T + 8 * V * (PACK - 1 - t), [P, 2, V], F32, "parts%d" % t) for t in late}
         mn_late = {t: tile([P, V], F32, "mn%d" % t) for t in late}
         mx_late = {t: tile([P, V], F32, "mx%d" % t) for t in late}
         a = [a_early[:, t, :] for t in early] + [ab[t][:, 0, :] for t in late]
@@ -180,28 +177,36 @@ def tile_picked_sortpair_relu_po_kernel(
         fetch_a(0)
         fetch_b(0)
         fetch_a(1)
-        fetch_b(1)
-        fetch_a(2)
         nc.vector.tensor_tensor(mn_early[:], a_early[:], b_early[:], ALU.min)
         nc.gpsimd.tensor_tensor(up_early[:], a_early[:], mn_early[:], ALU.subtract)
+        fetch_b(1)
+        fetch_a(2)
         fetch_b(2)
         fetch_a(3)
         fetch_b(3)
+        compare(1)
         nc.gpsimd.tensor_tensor(mx_early[:], b_early[:], up_early[:], ALU.add)
-        for t in late:
-            compare(t)
-        for t in early:
-            put_a(t)
-        for t in late:
-            larger(t)
-        for t in early:
-            put_b(t)
-            nc.scalar.copy(out=z_bf[:, :, t], in_=z[t][:])
-        for t in late:
-            put_b(t)
-        for t in late:
-            smaller(t)
+        put_a(0)
+        larger(1)
+        compare(2)
+        put_b(1)
+        compare(3)
+        put_b(0)
+        larger(2)
+        larger(3)
+        put_b(2)
+        put_b(3)
+        nc.scalar.copy(out=z_bf[:, :, 0], in_=z[0][:])
+        smaller(1)
+        put_a(1)
+        nc.scalar.copy(out=z_bf[:, :, 1], in_=z[1][:])
+        smaller(2)
         put_a(2)
+        smaller(3)
+        nc.gpsimd.tensor_copy(
+            out=w2_plane[:].rearrange("p (t m) -> p t m", t=PACK),
+            in_=w2s_raw[:].rearrange("p (m t) -> p t m", t=PACK),
+        )
         chunk = [slice(CHUNK * c, CHUNK * (c + 1)) for c in range(CHUNKS)]
         for c in range(CHUNKS):
             nc.scalar.copy(

@@ -24,6 +24,8 @@ HALF = S // 2
 CHUNK = 128
 CHUNKS = S // CHUNK
 M_SCALAR = 44
+AT_WORDS = 0
+AT_PARTS = 4 * T
 
 
 def tile_picked_sortpair_relu_po_kernel(
@@ -33,7 +35,6 @@ def tile_picked_sortpair_relu_po_kernel(
     with ExitStack() as ctx:
         keep = ctx.enter_context(tc.tile_pool(name="keep", bufs=1))
         psum = ctx.enter_context(tc.psum_pool(name="psum", bufs=8))
-
         shared = ctx.enter_context(tc.tile_pool(name="shared", bufs=1))
 
         def tile(shape, dtype, name):
@@ -48,7 +49,7 @@ def tile_picked_sortpair_relu_po_kernel(
         xs_table = tile([P, T], U8, "xs_table")
         xs_picked = tile([P, S], U8, "xs_picked")
         xs_plane = tile([P, S], U8, "xs_plane")
-        xw_table = tile_at(0, [P, T], U32, "xw_table")
+        xw_table = tile_at(AT_WORDS, [P, T], U32, "xw_table")
         xw_picked = tile([P, S], U32, "xw_picked")
         w1_raw = tile([P, PACK, H], F32, "w1_raw")
         w1_bf = tile([P, PACK * H], BF16, "w1_bf")
@@ -56,8 +57,8 @@ def tile_picked_sortpair_relu_po_kernel(
         w1_plane = tile([P, H], U8, "w1_plane")
         w2w_raw = tile([P, 2 * N], U8, "w2w_raw")
         w2s_raw = tile([P, N], U8, "w2s_raw")
-        w2_codes = tile_at(0, [P, 2 * N], U8, "w2_codes")
-        w2_plane = tile_at(4 * T, [P, N], U8, "w2_plane")
+        w2_codes = tile_at(AT_WORDS, [P, 2 * N], U8, "w2_codes")
+        w2_plane = tile_at(AT_PARTS, [P, N], U8, "w2_plane")
         warm_in = tile([P, 1], F32, "warm_in")
         warm_out = tile([P, 1], F32, "warm_out")
 
@@ -98,6 +99,11 @@ def tile_picked_sortpair_relu_po_kernel(
 
         y = [tile([P, S], F32, "y%d" % t) for t in range(PACK)]
 
+        def pick_words(cols):
+            nc.vector.tensor_copy(
+                xw_picked[:, cols], xw_table[:].indirect(offs_sb[:, cols.start // 16 : cols.stop // 16])
+            )
+
         def first_product(t, cols):
             width = cols.stop - cols.start
             bank = psum.tile([P, S], F32, name="bank")
@@ -113,13 +119,12 @@ def tile_picked_sortpair_relu_po_kernel(
             )
             nc.scalar.activation(out=y[t][:, cols], in_=bank[:, :width], func=RELU)
 
-        for h in range(2):
-            cols = slice(HALF * h, HALF * (h + 1))
-            nc.vector.tensor_copy(
-                xw_picked[:, cols], xw_table[:].indirect(offs_sb[:, HALF // 16 * h : HALF // 16 * (h + 1)])
-            )
-            for piece in ((cols,), (slice(HALF, HALF + CHUNK), slice(HALF + CHUNK, S)))[h]:
-                first_product(0, piece)
+        chunk = [slice(CHUNK * c, CHUNK * (c + 1)) for c in range(CHUNKS)]
+        pick_words(slice(0, HALF))
+        first_product(0, slice(0, HALF))
+        pick_words(slice(HALF, S))
+        first_product(0, chunk[2])
+        first_product(0, chunk[3])
         for t in range(1, PACK):
             first_product(t, slice(0, S))
 
@@ -128,24 +133,18 @@ def tile_picked_sortpair_relu_po_kernel(
             in_=w2w_raw[:].rearrange("p (m t b) -> p t m b", t=PACK, b=2),
         )
 
-        early = range(1)
-        late = range(1, PACK)
-        a_early = tile([P, 1, V], F32, "a_early")
-        b_early = tile([P, 1, V], F32, "b_early")
-        mn_early = tile([P, 1, V], F32, "mn_early")
-        up_early = tile([P, 1, V], F32, "up_early")
-        mx_early = tile([P, 1, V], F32, "mx_early")
-        ab = {t: tile([P, 2, V], F32, "ab%d" % t) for t in late}
-        diff = {t: tile([P, V], F32, "diff%d" % t) for t in late}
-        up = {t: tile([P, V], F32, "up%d" % t) for t in late}
-        take = {t: tile([P, 2, V], F32, "take%d" % t) for t in late}
-        parts = {t: tile_at(4 * T + 8 * V * (PACK - 1 - t), [P, 2, V], F32, "parts%d" % t) for t in late}
-        mn_late = {t: tile([P, V], F32, "mn%d" % t) for t in late}
-        mx_late = {t: tile([P, V], F32, "mx%d" % t) for t in late}
-        a = [a_early[:, t, :] for t in early] + [ab[t][:, 0, :] for t in late]
-        b = [b_early[:, t, :] for t in early] + [ab[t][:, 1, :] for t in late]
-        mn = [mn_early[:, t, :] for t in early] + [mn_late[t][:] for t in late]
-        mx = [mx_early[:, t, :] for t in early] + [mx_late[t][:] for t in late]
+        last = PACK - 1
+        by_masks = range(1, PACK)
+        ab = [tile([P, 2, V], F32, "ab%d" % t) for t in range(PACK)]
+        a = [ab[t][:, 0, :] for t in range(PACK)]
+        b = [ab[t][:, 1, :] for t in range(PACK)]
+        up = [tile([P, V], F32, "up%d" % t) for t in range(PACK)]
+        mn = [tile([P, V], F32, "mn%d" % t) for t in range(PACK)]
+        mx = [tile([P, V], F32, "mx%d" % t) for t in range(PACK)]
+        diff = {t: tile([P, V], F32, "diff%d" % t) for t in by_masks}
+        take = {t: tile([P, 2, V], F32, "take%d" % t) for t in by_masks}
+        parts = {t: tile([P, 2, V], F32, "parts%d" % t) for t in range(1, last)}
+        parts[last] = tile_at(AT_PARTS, [P, 2, V], F32, "parts%d" % last)
         z = [tile([P, S], F32, "z%d" % t) for t in range(PACK)]
         z_bf = tile([P, S, PACK], BF16, "z_bf")
 
@@ -162,57 +161,61 @@ def tile_picked_sortpair_relu_po_kernel(
             nc.scalar.activation(out=take[t][:, 0, :], in_=take[t][:, 1, :], func=RELU, scale=-1.0, bias=1.0)
 
         def larger(t):
-            nc.gpsimd.tensor_tensor(mx[t], b[t], up[t][:], ALU.add)
+            nc.gpsimd.tensor_tensor(mx[t][:], b[t], up[t][:], ALU.add)
 
         def smaller(t):
             nc.gpsimd.tensor_tensor(parts[t][:], ab[t][:], take[t][:], ALU.mult)
-            nc.gpsimd.tensor_tensor(mn[t], parts[t][:, 0, :], parts[t][:, 1, :], ALU.add)
+            nc.gpsimd.tensor_tensor(mn[t][:], parts[t][:, 0, :], parts[t][:, 1, :], ALU.add)
 
         def put_a(t):
-            nc.vector.tensor_copy(z[t][:].indirect(la_sb[:]), mn[t])
+            nc.vector.tensor_copy(z[t][:].indirect(la_sb[:]), mn[t][:])
 
         def put_b(t):
-            nc.vector.tensor_copy(z[t][:].indirect(lb_sb[:]), mx[t])
+            nc.vector.tensor_copy(z[t][:].indirect(lb_sb[:]), mx[t][:])
+
+        def round_z(copy, t, cols):
+            copy(out=z_bf[:, cols, t], in_=z[t][:, cols])
 
         fetch_a(0)
         fetch_b(0)
         fetch_a(1)
-        nc.vector.tensor_tensor(mn_early[:], a_early[:], b_early[:], ALU.min)
-        nc.gpsimd.tensor_tensor(up_early[:], a_early[:], mn_early[:], ALU.subtract)
+        nc.vector.tensor_tensor(mn[0][:], a[0], b[0], ALU.min)
+        nc.gpsimd.tensor_tensor(up[0][:], a[0], mn[0][:], ALU.subtract)
         fetch_b(1)
-        fetch_a(2)
-        fetch_b(2)
-        fetch_a(3)
-        fetch_b(3)
+        for t in range(2, PACK):
+            fetch_a(t)
+            fetch_b(t)
         compare(1)
-        nc.gpsimd.tensor_tensor(mx_early[:], b_early[:], up_early[:], ALU.add)
+        larger(0)
         put_a(0)
         larger(1)
         compare(2)
         put_b(1)
         compare(3)
         put_b(0)
-        larger(2)
-        larger(3)
-        put_b(2)
-        put_b(3)
-        nc.scalar.copy(out=z_bf[:, :, 0], in_=z[0][:])
-        smaller(1)
-        put_a(1)
-        nc.scalar.copy(out=z_bf[:, :, 1], in_=z[1][:])
-        smaller(2)
-        put_a(2)
-        smaller(3)
+        for t in range(2, PACK):
+            larger(t)
+        for t in range(2, PACK):
+            put_b(t)
+        for t in range(1, last):
+            round_z(nc.scalar.copy, t - 1, slice(0, S))
+            smaller(t)
+            put_a(t)
+        smaller(last)
+
         nc.gpsimd.tensor_copy(
             out=w2_plane[:].rearrange("p (t m) -> p t m", t=PACK),
             in_=w2s_raw[:].rearrange("p (m t) -> p t m", t=PACK),
         )
-        chunk = [slice(CHUNK * c, CHUNK * (c + 1)) for c in range(CHUNKS)]
+
         for c in range(CHUNKS):
-            nc.scalar.copy(
-                out=z_bf[:, chunk[c], 2:4], in_=z[2][:, chunk[c]].unsqueeze(2).to_broadcast([P, CHUNK, 2])
-            )
-        put_a(3)
+            if c % 2:
+                round_z(nc.scalar.copy, 2, chunk[c])
+            else:
+                nc.scalar.copy(
+                    out=z_bf[:, chunk[c], 2:4], in_=z[2][:, chunk[c]].unsqueeze(2).to_broadcast([P, CHUNK, 2])
+                )
+        put_a(last)
 
         z_codes = tile([P, S], U32, "z_codes")
         z_plane = tile([P, S], U8, "z_plane")
@@ -224,10 +227,6 @@ def tile_picked_sortpair_relu_po_kernel(
         o_f32 = [tile([P, PACK, CHUNK], F32, "o_f32_%d" % c) for c in range(CHUNKS)]
         o_bf = [tile([P, CHUNK, PACK], BF16, "o_bf_%d" % c) for c in range(CHUNKS)]
 
-        def finish_z(c):
-            copy = nc.scalar.copy if c % 2 else nc.vector.tensor_copy
-            copy(out=z_bf[:, chunk[c], 3], in_=z[3][:, chunk[c]])
-
         def second_product(c):
             nc.vector.quantize_mx(
                 out=z_codes[:, chunk[c]].bitcast(FP8X4),
@@ -237,9 +236,9 @@ def tile_picked_sortpair_relu_po_kernel(
             per_bank = 2 if c == 0 else PACK
             banks[c] = [psum.tile([P, S], F32, name="bank") for u in range(PACK // per_bank)]
             for t in range(PACK):
-                slot = t % per_bank
+                at = CHUNK * (t % per_bank)
                 nc.tensor.matmul_mx(
-                    out=banks[c][t // per_bank][:, CHUNK * slot : CHUNK * (slot + 1)],
+                    out=banks[c][t // per_bank][:, at : at + CHUNK],
                     lhsT=w2_codes[:, 2 * P * t : 2 * P * (t + 1)].bitcast(FP4X4),
                     lhsT_scale=w2_plane[:, P * t : P * (t + 1)],
                     rhs=z_codes[:, chunk[c]].bitcast(FP8X4),
@@ -278,7 +277,7 @@ def tile_picked_sortpair_relu_po_kernel(
             nc.sync.dma_start(out=words_dst[:, cols], in_=o_codes[:, cols].bitcast(I32))
 
         for c in range(CHUNKS):
-            finish_z(c)
+            round_z(nc.scalar.copy if c % 2 else nc.vector.tensor_copy, last, chunk[c])
         for c in range(CHUNKS):
             second_product(c)
         leave_f32_halves(0)

@@ -25,7 +25,7 @@ CHUNK = 128
 CHUNKS = S // CHUNK
 M_SCALAR = 44
 AT_WORDS = 0
-AT_PARTS = 4 * T
+AT_W1 = 4 * T
 
 
 def tile_picked_sortpair_relu_po_kernel(
@@ -52,13 +52,13 @@ def tile_picked_sortpair_relu_po_kernel(
         xw_table = tile_at(AT_WORDS, [P, T], U32, "xw_table")
         xw_picked = tile([P, S], U32, "xw_picked")
         w1_raw = tile([P, PACK, H], F32, "w1_raw")
-        w1_bf = tile([P, PACK * H], BF16, "w1_bf")
+        w1_bf = tile_at(AT_W1, [P, PACK * H], BF16, "w1_bf")
         w1_codes = tile([P, H], U32, "w1_codes")
         w1_plane = tile([P, H], U8, "w1_plane")
         w2w_raw = tile([P, 2 * N], U8, "w2w_raw")
         w2s_raw = tile([P, N], U8, "w2s_raw")
         w2_codes = tile_at(AT_WORDS, [P, 2 * N], U8, "w2_codes")
-        w2_plane = tile_at(AT_PARTS, [P, N], U8, "w2_plane")
+        w2_plane = tile_at(AT_W1, [P, N], U8, "w2_plane")
         warm_in = tile([P, 1], F32, "warm_in")
         warm_out = tile([P, 1], F32, "warm_out")
 
@@ -96,6 +96,11 @@ def tile_picked_sortpair_relu_po_kernel(
         nc.scalar.copy(out=w1_dst[:, :M_SCALAR], in_=w1_src[:, :M_SCALAR])
         nc.vector.tensor_copy(out=w1_dst[:, M_SCALAR:], in_=w1_src[:, M_SCALAR:])
         nc.vector.quantize_mx(out=w1_codes[:].bitcast(FP8X4), scales=w1_plane[:], in_=w1_bf[:])
+
+        nc.gpsimd.tensor_copy(
+            out=w2_plane[:].rearrange("p (t m) -> p t m", t=PACK),
+            in_=w2s_raw[:].rearrange("p (m t) -> p t m", t=PACK),
+        )
 
         y = [tile([P, S], F32, "y%d" % t) for t in range(PACK)]
 
@@ -143,8 +148,7 @@ def tile_picked_sortpair_relu_po_kernel(
         mx = [tile([P, V], F32, "mx%d" % t) for t in range(PACK)]
         diff = {t: tile([P, V], F32, "diff%d" % t) for t in by_masks}
         take = {t: tile([P, 2, V], F32, "take%d" % t) for t in by_masks}
-        parts = {t: tile([P, 2, V], F32, "parts%d" % t) for t in range(1, last)}
-        parts[last] = tile_at(AT_PARTS, [P, 2, V], F32, "parts%d" % last)
+        parts = {t: tile([P, 2, V], F32, "parts%d" % t) for t in by_masks}
         z = [tile([P, S], F32, "z%d" % t) for t in range(PACK)]
         z_bf = tile([P, S, PACK], BF16, "z_bf")
 
@@ -202,11 +206,6 @@ def tile_picked_sortpair_relu_po_kernel(
             smaller(t)
             put_a(t)
         smaller(last)
-
-        nc.gpsimd.tensor_copy(
-            out=w2_plane[:].rearrange("p (t m) -> p t m", t=PACK),
-            in_=w2s_raw[:].rearrange("p (m t) -> p t m", t=PACK),
-        )
 
         for c in range(CHUNKS):
             if c % 2:

@@ -24,8 +24,11 @@ HALF = S // 2
 CHUNK = 128
 CHUNKS = S // CHUNK
 M_SCALAR = 44
-AT_WORDS = 0
-AT_W1 = 4 * T
+AT_PARTS = 0
+AT_UP0 = AT_PARTS + 8 * V + 2 * V
+AT_UP1 = AT_UP0 + 2 * V + 4 * V
+AT_W1 = AT_UP1 + 4 * S
+AT_SCALES = AT_W1 + 2 * PACK * H
 
 
 def tile_picked_sortpair_relu_po_kernel(
@@ -46,39 +49,38 @@ def tile_picked_sortpair_relu_po_kernel(
         offs_sb = tile([P, S // 16], U16, "offs_sb")
         la_sb = tile([P, V // 16], U16, "la_sb")
         lb_sb = tile([P, V // 16], U16, "lb_sb")
-        xs_table = tile([P, T], U8, "xs_table")
+        xs_table = tile_at(AT_SCALES, [P, T], U8, "xs_table")
         xs_picked = tile([P, S], U8, "xs_picked")
         xs_plane = tile([P, S], U8, "xs_plane")
-        xw_table = tile_at(AT_WORDS, [P, T], U32, "xw_table")
+        xw_table = tile([P, T], U32, "xw_table")
         xw_picked = tile([P, S], U32, "xw_picked")
         w1_raw = tile([P, PACK, H], F32, "w1_raw")
         w1_bf = tile_at(AT_W1, [P, PACK * H], BF16, "w1_bf")
         w1_codes = tile([P, H], U32, "w1_codes")
         w1_plane = tile([P, H], U8, "w1_plane")
-        w2w_raw = tile([P, 2 * N], U8, "w2w_raw")
+        w2w_raw = tile_at(AT_SCALES, [P, 2 * N], U8, "w2w_raw")
         w2s_raw = tile([P, N], U8, "w2s_raw")
-        w2_codes = tile_at(AT_WORDS, [P, 2 * N], U8, "w2_codes")
+        w2_codes = tile_at(AT_PARTS, [P, 2 * N], U8, "w2_codes")
         w2_plane = tile_at(AT_W1, [P, N], U8, "w2_plane")
         warm_in = tile([P, 1], F32, "warm_in")
         warm_out = tile([P, 1], F32, "warm_out")
 
+        nc.gpsimd.memset(xs_table[:].bitcast(I32), 0)
         nc.vector.memset(warm_in[:], 0.0)
         nc.vector.memset(xs_plane[:].bitcast(I32), 0)
         nc.gpsimd.memset(w2s_raw[:].bitcast(I32), 0)
 
+        w1_rows = w1.rearrange("(p j) c -> p j c", j=PACK)
+        nc.sync.dma_start(out=w1_raw[:, :1], in_=w1_rows[:, :1])
         nc.sync.dma_start(offs_sb[:], offs)
-        nc.scalar.dma_start(
-            out=xs_table[:].bitcast(I32),
-            in_=x_scales[0].bitcast(I32).unsqueeze(1).to_broadcast([16, 8, T // 4]),
-        )
-        nc.scalar.activation(out=warm_out[:], in_=warm_in[:], func=RELU)
         nc.sync.dma_start(la_sb[:], la)
-        nc.sync.dma_start(out=w1_raw[:], in_=w1.rearrange("(p j) c -> p j c", j=PACK))
+        nc.sync.dma_start(out=xs_table[0:P:8, :].bitcast(I32), in_=x_scales[0].bitcast(I32))
+        nc.scalar.activation(out=warm_out[:], in_=warm_in[:], func=RELU)
+        nc.sync.dma_start(out=w1_raw[:, 1:], in_=w1_rows[:, 1:])
         nc.sync.dma_start(
             out=xw_table[:].bitcast(I32), in_=x_words[0].rearrange("p c r -> p (c r)").bitcast(I32)
         )
         nc.sync.dma_start(lb_sb[:], lb)
-        nc.sync.dma_start(out=w2w_raw[:].bitcast(I32), in_=w2_words[0].bitcast(I32))
         for q in range(QUADS):
             nc.gpsimd.dma_start(
                 out=w2s_raw[32 * q : 32 * q + 4, :].bitcast(I32), in_=w2_scales[0][4 * q : 4 * q + 4, :].bitcast(I32)
@@ -86,10 +88,12 @@ def tile_picked_sortpair_relu_po_kernel(
 
         nc.vector.tensor_copy(xs_picked[:], xs_table[:].indirect(offs_sb[:]))
         for q in range(QUADS):
-            nc.scalar.dma_start(
+            queue = nc.scalar if q % 2 else nc.sync
+            queue.dma_start(
                 out=xs_plane[32 * q : 32 * q + 4, :].bitcast(I32),
                 in_=xs_picked[32 * q : 32 * q + 32 : 8, :].bitcast(I32),
             )
+        nc.sync.dma_start(out=w2w_raw[:].bitcast(I32), in_=w2_words[0].bitcast(I32))
 
         w1_dst = w1_bf[:].rearrange("p (t m j) -> p m j t", t=PACK, j=PACK)
         w1_src = w1_raw[:].rearrange("p j (m t) -> p m j t", t=PACK)
@@ -133,29 +137,28 @@ def tile_picked_sortpair_relu_po_kernel(
         for t in range(1, PACK):
             first_product(t, slice(0, S))
 
-        nc.vector.tensor_copy(
-            out=w2_codes[:].rearrange("p (t m b) -> p t m b", t=PACK, b=2),
-            in_=w2w_raw[:].rearrange("p (m t b) -> p t m b", t=PACK, b=2),
-        )
-
-        last = PACK - 1
-        by_masks = range(1, PACK)
+        by_min = PACK - 1
+        by_masks = range(by_min)
+        last = by_min - 1
         ab = [tile([P, 2, V], F32, "ab%d" % t) for t in range(PACK)]
         a = [ab[t][:, 0, :] for t in range(PACK)]
         b = [ab[t][:, 1, :] for t in range(PACK)]
-        up = [tile([P, V], F32, "up%d" % t) for t in range(PACK)]
-        mn = [tile([P, V], F32, "mn%d" % t) for t in range(PACK)]
+        up = [tile([P, V], F32, "up%d" % t) for t in range(2, PACK)]
+        up = [tile_at(AT_UP0, [P, V], F32, "up0"), tile_at(AT_UP1, [P, V], F32, "up1")] + up
+        mn = [tile([P, V], F32, "mn%d" % t) for t in by_masks]
+        mn.append(tile_at(AT_UP0 + 2 * V, [P, V], F32, "mn3"))
         mx = [tile([P, V], F32, "mx%d" % t) for t in range(PACK)]
-        diff = {t: tile([P, V], F32, "diff%d" % t) for t in by_masks}
-        take = {t: tile([P, 2, V], F32, "take%d" % t) for t in by_masks}
-        parts = {t: tile([P, 2, V], F32, "parts%d" % t) for t in by_masks}
-        z = [tile([P, S], F32, "z%d" % t) for t in range(PACK)]
+        diff = [tile([P, V], F32, "diff%d" % t) for t in range(last)]
+        diff.append(tile_at(AT_UP0 - 2 * V, [P, V], F32, "diff2"))
+        take = [tile([P, 2, V], F32, "take%d" % t) for t in by_masks]
+        parts = [tile([P, 2, V], F32, "parts%d" % t) for t in range(last)]
+        parts.append(tile_at(AT_PARTS, [P, 2, V], F32, "parts2"))
+        z = [tile([P, S], F32, "z%d" % t) for t in by_masks]
+        z.append(tile_at(AT_UP1, [P, S], F32, "z3"))
         z_bf = tile([P, S, PACK], BF16, "z_bf")
 
-        def fetch_a(t):
+        def fetch(t):
             nc.vector.tensor_copy(a[t], y[t][:].indirect(la_sb[:]))
-
-        def fetch_b(t):
             nc.vector.tensor_copy(b[t], y[t][:].indirect(lb_sb[:]))
 
         def compare(t):
@@ -167,8 +170,10 @@ def tile_picked_sortpair_relu_po_kernel(
         def larger(t):
             nc.gpsimd.tensor_tensor(mx[t][:], b[t], up[t][:], ALU.add)
 
-        def smaller(t):
+        def products(t):
             nc.gpsimd.tensor_tensor(parts[t][:], ab[t][:], take[t][:], ALU.mult)
+
+        def smaller(t):
             nc.gpsimd.tensor_tensor(mn[t][:], parts[t][:, 0, :], parts[t][:, 1, :], ALU.add)
 
         def put_a(t):
@@ -180,41 +185,39 @@ def tile_picked_sortpair_relu_po_kernel(
         def round_z(copy, t, cols):
             copy(out=z_bf[:, cols, t], in_=z[t][:, cols])
 
-        fetch_a(0)
-        fetch_b(0)
-        fetch_a(1)
-        nc.vector.tensor_tensor(mn[0][:], a[0], b[0], ALU.min)
-        nc.gpsimd.tensor_tensor(up[0][:], a[0], mn[0][:], ALU.subtract)
-        fetch_b(1)
-        for t in range(2, PACK):
-            fetch_a(t)
-            fetch_b(t)
+        for t in range(PACK):
+            fetch(t)
+        compare(0)
         compare(1)
         larger(0)
-        put_a(0)
-        larger(1)
-        compare(2)
-        put_b(1)
-        compare(3)
         put_b(0)
-        for t in range(2, PACK):
-            larger(t)
-        for t in range(2, PACK):
-            put_b(t)
-        for t in range(1, last):
-            round_z(nc.scalar.copy, t - 1, slice(0, S))
+        nc.vector.tensor_tensor(mn[by_min][:], a[by_min], b[by_min], ALU.min)
+        larger(1)
+        put_b(1)
+        put_a(by_min)
+        compare(2)
+        products(0)
+        larger(2)
+        put_b(2)
+        nc.gpsimd.tensor_tensor(up[by_min][:], a[by_min], mn[by_min][:], ALU.subtract)
+        smaller(0)
+        put_a(0)
+        larger(by_min)
+        put_b(by_min)
+        round_z(nc.scalar.copy, 0, slice(0, S))
+        nc.scalar.copy(out=z_bf[:, :, 2:4], in_=z[by_min][:].unsqueeze(2).to_broadcast([P, S, 2]))
+        for t in range(1, by_min):
+            products(t)
+        for t in range(1, by_min):
             smaller(t)
             put_a(t)
-        smaller(last)
+        for cols in (slice(0, HALF), slice(HALF, S)):
+            round_z(nc.scalar.copy, 1, cols)
 
-        for c in range(CHUNKS):
-            if c % 2:
-                round_z(nc.scalar.copy, 2, chunk[c])
-            else:
-                nc.scalar.copy(
-                    out=z_bf[:, chunk[c], 2:4], in_=z[2][:, chunk[c]].unsqueeze(2).to_broadcast([P, CHUNK, 2])
-                )
-        put_a(last)
+        nc.gpsimd.tensor_copy(
+            out=w2_codes[:].rearrange("p (t m b) -> p t m b", t=PACK, b=2),
+            in_=w2w_raw[:].rearrange("p (m t b) -> p t m b", t=PACK, b=2),
+        )
 
         z_codes = tile([P, S], U32, "z_codes")
         z_plane = tile([P, S], U8, "z_plane")
@@ -232,7 +235,7 @@ def tile_picked_sortpair_relu_po_kernel(
                 scales=z_plane[:, chunk[c]],
                 in_=z_bf[:, chunk[c], :].rearrange("p c t -> p (c t)"),
             )
-            per_bank = 2 if c == 0 else PACK
+            per_bank = 2
             banks[c] = [psum.tile([P, S], F32, name="bank") for u in range(PACK // per_bank)]
             for t in range(PACK):
                 at = CHUNK * (t % per_bank)
@@ -246,24 +249,19 @@ def tile_picked_sortpair_relu_po_kernel(
                     stop=True,
                 )
 
-        def leave_f32(c, queue):
-            nc.scalar.copy(out=o_f32[c][:].rearrange("p t c -> p (t c)"), in_=banks[c][0][:])
-            queue.dma_start(out=out_rows[:, :, chunk[c]], in_=o_f32[c][:])
+        def leave_half(c, u, copy):
+            rows = slice(2 * u, 2 * u + 2)
+            copy(out=o_f32[c][:, rows, :].rearrange("p t c -> p (t c)"), in_=banks[c][u][:, : 2 * CHUNK])
 
-        def leave_f32_halves(c):
-            for u, copy in enumerate((nc.scalar.copy, nc.vector.tensor_copy)):
-                rows = slice(2 * u, 2 * u + 2)
-                copy(out=o_f32[c][:, rows, :].rearrange("p t c -> p (t c)"), in_=banks[c][u][:, : 2 * CHUNK])
-                nc.sync.dma_start(out=out_rows[:, rows, chunk[c]], in_=o_f32[c][:, rows, :])
+        def store_half(c, u):
+            rows = slice(2 * u, 2 * u + 2)
+            nc.sync.dma_start(out=out_rows[:, rows, chunk[c]], in_=o_f32[c][:, rows, :])
 
         def weave_from_sbuf(c):
             nc.vector.tensor_copy(
                 out=o_bf[c][:].rearrange("p (g i) t -> p g t i", i=4),
                 in_=o_f32[c][:].rearrange("p t (g i) -> p g t i", i=4),
             )
-
-        def weave_from_psum(c):
-            nc.scalar.copy(out=o_bf[c][:], in_=banks[c][0][:].rearrange("p (t c) -> p c t", t=PACK))
 
         def leave_codes(c):
             nc.vector.quantize_mx(
@@ -279,19 +277,21 @@ def tile_picked_sortpair_relu_po_kernel(
             round_z(nc.scalar.copy if c % 2 else nc.vector.tensor_copy, last, chunk[c])
         for c in range(CHUNKS):
             second_product(c)
-        leave_f32_halves(0)
+        leave_half(0, 0, nc.scalar.copy)
+        store_half(0, 0)
+        leave_half(0, 1, nc.vector.tensor_copy)
+        store_half(0, 1)
         weave_from_sbuf(0)
-        leave_f32(1, nc.sync)
-        leave_codes(0)
-        weave_from_sbuf(1)
-        leave_f32(2, nc.sync)
-        leave_codes(1)
-        store_words(slice(0, HALF))
-        weave_from_psum(3)
-        weave_from_sbuf(2)
-        leave_f32(3, nc.scalar)
-        leave_codes(2)
-        leave_codes(3)
+        for c in range(1, CHUNKS):
+            for u in range(2):
+                leave_half(c, u, nc.scalar.copy)
+            queue = nc.scalar if c == CHUNKS - 1 else nc.sync
+            queue.dma_start(out=out_rows[:, :, chunk[c]], in_=o_f32[c][:])
+            weave_from_sbuf(c)
+            leave_codes(c - 1)
+            if c == 2:
+                store_words(slice(0, HALF))
+        leave_codes(CHUNKS - 1)
         store_words(slice(HALF, S))
         for q in range(QUADS):
             queue = nc.scalar if q % 2 else nc.sync

@@ -23,12 +23,13 @@ QUADS = 4
 HALF = S // 2
 CHUNK = 128
 CHUNKS = S // CHUNK
-M_SCALAR = 44
+M_SCALAR = 36
 AT_PARTS = 0
 AT_UP0 = AT_PARTS + 8 * V + 2 * V
 AT_UP1 = AT_UP0 + 2 * V + 4 * V
 AT_W1 = AT_UP1 + 4 * S
 AT_SCALES = AT_W1 + 2 * PACK * H
+AT_WORDS = AT_SCALES + T
 
 
 def tile_picked_sortpair_relu_po_kernel(
@@ -52,11 +53,12 @@ def tile_picked_sortpair_relu_po_kernel(
         xs_table = tile_at(AT_SCALES, [P, T], U8, "xs_table")
         xs_picked = tile([P, S], U8, "xs_picked")
         xs_plane = tile([P, S], U8, "xs_plane")
-        xw_table = tile([P, T], U32, "xw_table")
+        xw_table = tile_at(AT_WORDS, [P, T], U32, "xw_table")
         xw_picked = tile([P, S], U32, "xw_picked")
         w1_raw = tile([P, PACK, H], F32, "w1_raw")
         w1_bf = tile_at(AT_W1, [P, PACK * H], BF16, "w1_bf")
-        w1_codes = tile([P, H], U32, "w1_codes")
+        w1_codes = tile([P, P], U32, "w1_codes")
+        w1_later = tile_at(AT_WORDS, [P, H - P], U32, "w1_later")
         w1_plane = tile([P, H], U8, "w1_plane")
         w2w_raw = tile_at(AT_SCALES, [P, 2 * N], U8, "w2w_raw")
         w2s_raw = tile([P, N], U8, "w2s_raw")
@@ -88,8 +90,7 @@ def tile_picked_sortpair_relu_po_kernel(
 
         nc.vector.tensor_copy(xs_picked[:], xs_table[:].indirect(offs_sb[:]))
         for q in range(QUADS):
-            queue = nc.scalar if q % 2 else nc.sync
-            queue.dma_start(
+            nc.sync.dma_start(
                 out=xs_plane[32 * q : 32 * q + 4, :].bitcast(I32),
                 in_=xs_picked[32 * q : 32 * q + 32 : 8, :].bitcast(I32),
             )
@@ -99,12 +100,20 @@ def tile_picked_sortpair_relu_po_kernel(
         w1_src = w1_raw[:].rearrange("p j (m t) -> p m j t", t=PACK)
         nc.scalar.copy(out=w1_dst[:, :M_SCALAR], in_=w1_src[:, :M_SCALAR])
         nc.vector.tensor_copy(out=w1_dst[:, M_SCALAR:], in_=w1_src[:, M_SCALAR:])
-        nc.vector.quantize_mx(out=w1_codes[:].bitcast(FP8X4), scales=w1_plane[:], in_=w1_bf[:])
 
-        nc.gpsimd.tensor_copy(
-            out=w2_plane[:].rearrange("p (t m) -> p t m", t=PACK),
-            in_=w2s_raw[:].rearrange("p (m t) -> p t m", t=PACK),
-        )
+        def w1_words(first, count):
+            if first == 0:
+                return w1_codes[:].bitcast(FP8X4)
+            return w1_later[:, P * (first - 1) : P * (first - 1 + count)].bitcast(FP8X4)
+
+        def quantise_w1(first, count):
+            nc.vector.quantize_mx(
+                out=w1_words(first, count),
+                scales=w1_plane[:, P * first : P * (first + count)],
+                in_=w1_bf[:, PACK * P * first : PACK * P * (first + count)],
+            )
+
+        quantise_w1(0, 1)
 
         y = [tile([P, S], F32, "y%d" % t) for t in range(PACK)]
 
@@ -119,7 +128,7 @@ def tile_picked_sortpair_relu_po_kernel(
             rows = slice(P * t, P * (t + 1))
             nc.tensor.matmul_mx(
                 out=bank[:, :width],
-                lhsT=w1_codes[:, rows].bitcast(FP8X4),
+                lhsT=w1_words(t, 1),
                 lhsT_scale=w1_plane[:, rows],
                 rhs=xw_picked[:, cols].bitcast(FP8X4),
                 rhs_scale=xs_plane[:, cols],
@@ -134,8 +143,15 @@ def tile_picked_sortpair_relu_po_kernel(
         pick_words(slice(HALF, S))
         first_product(0, chunk[2])
         first_product(0, chunk[3])
+        quantise_w1(1, 1)
+        quantise_w1(2, 2)
         for t in range(1, PACK):
             first_product(t, slice(0, S))
+
+        nc.gpsimd.tensor_copy(
+            out=w2_plane[:].rearrange("p (t m) -> p t m", t=PACK),
+            in_=w2s_raw[:].rearrange("p (m t) -> p t m", t=PACK),
+        )
 
         by_min = PACK - 1
         by_masks = range(by_min)

@@ -90,7 +90,7 @@ def tile_picked_sortpair_relu_po_kernel(
 
         nc.vector.tensor_copy(xs_picked[:], xs_table[:].indirect(offs_sb[:]))
         for q in range(QUADS):
-            nc.sync.dma_start(
+            nc.scalar.dma_start(
                 out=xs_plane[32 * q : 32 * q + 4, :].bitcast(I32),
                 in_=xs_picked[32 * q : 32 * q + 32 : 8, :].bitcast(I32),
             )

@@ -23,7 +23,6 @@ QUADS = 4
 HALF = S // 2
 CHUNK = 128
 CHUNKS = S // CHUNK
-M_SCALAR = 36
 AT_PARTS = 0
 AT_UP0 = AT_PARTS + 8 * V + 2 * V
 AT_UP1 = AT_UP0 + 2 * V + 4 * V
@@ -64,21 +63,17 @@ def tile_picked_sortpair_relu_po_kernel(
         w2s_raw = tile([P, N], U8, "w2s_raw")
         w2_codes = tile_at(AT_PARTS, [P, 2 * N], U8, "w2_codes")
         w2_plane = tile_at(AT_W1, [P, N], U8, "w2_plane")
-        warm_in = tile([P, 1], F32, "warm_in")
-        warm_out = tile([P, 1], F32, "warm_out")
 
         nc.gpsimd.memset(xs_table[:].bitcast(I32), 0)
-        nc.vector.memset(warm_in[:], 0.0)
         nc.vector.memset(xs_plane[:].bitcast(I32), 0)
         nc.gpsimd.memset(w2s_raw[:].bitcast(I32), 0)
 
         w1_rows = w1.rearrange("(p j) c -> p j c", j=PACK)
-        nc.sync.dma_start(out=w1_raw[:, :1], in_=w1_rows[:, :1])
+        nc.sync.dma_start(out=w1_raw[:, :2], in_=w1_rows[:, :2])
         nc.sync.dma_start(offs_sb[:], offs)
         nc.sync.dma_start(la_sb[:], la)
         nc.sync.dma_start(out=xs_table[0:P:8, :].bitcast(I32), in_=x_scales[0].bitcast(I32))
-        nc.scalar.activation(out=warm_out[:], in_=warm_in[:], func=RELU)
-        nc.sync.dma_start(out=w1_raw[:, 1:], in_=w1_rows[:, 1:])
+        nc.sync.dma_start(out=w1_raw[:, 2:], in_=w1_rows[:, 2:])
         nc.sync.dma_start(
             out=xw_table[:].bitcast(I32), in_=x_words[0].rearrange("p c r -> p (c r)").bitcast(I32)
         )
@@ -98,8 +93,7 @@ def tile_picked_sortpair_relu_po_kernel(
 
         w1_dst = w1_bf[:].rearrange("p (t m j) -> p m j t", t=PACK, j=PACK)
         w1_src = w1_raw[:].rearrange("p j (m t) -> p m j t", t=PACK)
-        nc.scalar.copy(out=w1_dst[:, :M_SCALAR], in_=w1_src[:, :M_SCALAR])
-        nc.vector.tensor_copy(out=w1_dst[:, M_SCALAR:], in_=w1_src[:, M_SCALAR:])
+        nc.vector.tensor_copy(out=w1_dst, in_=w1_src)
 
         def w1_words(first, count):
             if first == 0:

@@ -23,6 +23,7 @@ QUADS = 4
 HALF = S // 2
 CHUNK = 128
 CHUNKS = S // CHUNK
+CLEARED = T // 2
 AT_PARTS = 0
 AT_UP0 = AT_PARTS + 8 * V + 2 * V
 AT_UP1 = AT_UP0 + 2 * V + 4 * V
@@ -64,19 +65,24 @@ def tile_picked_sortpair_relu_po_kernel(
         w2_codes = tile_at(AT_PARTS, [P, 2 * N], U8, "w2_codes")
         w2_plane = tile_at(AT_W1, [P, N], U8, "w2_plane")
 
-        nc.gpsimd.memset(xs_table[:].bitcast(I32), 0)
+        nc.gpsimd.memset(xs_table[:, :CLEARED].bitcast(I32), 0)
         nc.vector.memset(xs_plane[:].bitcast(I32), 0)
         nc.gpsimd.memset(w2s_raw[:].bitcast(I32), 0)
 
+        xs_rows = x_scales[0].bitcast(I32)
         w1_rows = w1.rearrange("(p j) c -> p j c", j=PACK)
-        nc.sync.dma_start(out=w1_raw[:, :2], in_=w1_rows[:, :2])
+        nc.sync.dma_start(
+            out=xs_table[:, CLEARED:].bitcast(I32),
+            in_=xs_rows[:, CLEARED // 4 :].unsqueeze(1).to_broadcast([16, 8, (T - CLEARED) // 4]),
+        )
+        nc.sync.dma_start(out=w1_raw[:, :1], in_=w1_rows[:, :1])
         nc.sync.dma_start(offs_sb[:], offs)
-        nc.sync.dma_start(la_sb[:], la)
-        nc.sync.dma_start(out=xs_table[0:P:8, :].bitcast(I32), in_=x_scales[0].bitcast(I32))
-        nc.sync.dma_start(out=w1_raw[:, 2:], in_=w1_rows[:, 2:])
+        nc.sync.dma_start(out=xs_table[0:P:8, :CLEARED].bitcast(I32), in_=xs_rows[:, : CLEARED // 4])
+        nc.sync.dma_start(out=w1_raw[:, 1:], in_=w1_rows[:, 1:])
         nc.sync.dma_start(
             out=xw_table[:].bitcast(I32), in_=x_words[0].rearrange("p c r -> p (c r)").bitcast(I32)
         )
+        nc.sync.dma_start(la_sb[:], la)
         nc.sync.dma_start(lb_sb[:], lb)
         for q in range(QUADS):
             nc.gpsimd.dma_start(

@@ -15,7 +15,7 @@ FP8X4 = mybir.dt.float8_e4m3fn_x4
 FP4X4 = mybir.dt.float4_e2m1fn_x4
 ALU = mybir.AluOpType
 RELU = mybir.ActivationFunctionType.Relu
-SIGN = mybir.ActivationFunctionType.Sign
+COPY = mybir.ActivationFunctionType.Copy
 
 P = 128
 PACK = 4
@@ -24,11 +24,15 @@ HALF = S // 2
 CHUNK = 128
 CHUNKS = S // CHUNK
 CLEARED = T // 2
-AT_PARTS = 0
-AT_UP0 = AT_PARTS + 8 * V + 2 * V
-AT_UP1 = AT_UP0 + 2 * V + 4 * V
-AT_W1 = AT_UP1 + 4 * S
-AT_SCALES = AT_W1 + 2 * PACK * H
+ORDER = (1, 2, 3, 0)
+AT_Z0 = 0
+AT_UP0 = AT_Z0 + 4 * S
+AT_UP1 = AT_UP0 + 4 * S
+AT_Y2 = AT_UP1 + 4 * V
+AT_Y3 = AT_Y2 + 4 * V
+AT_UP3 = AT_Y3 + 4 * V + 2 * PACK * S
+AT_B3 = AT_UP3 + 4 * V
+AT_SCALES = AT_B3 + 4 * V
 AT_WORDS = AT_SCALES + T
 
 
@@ -38,7 +42,7 @@ def tile_picked_sortpair_relu_po_kernel(
     nc = tc.nc
     with ExitStack() as ctx:
         keep = ctx.enter_context(tc.tile_pool(name="keep", bufs=1))
-        psum = ctx.enter_context(tc.psum_pool(name="psum", bufs=8))
+        psum = ctx.enter_context(tc.psum_pool(name="psum", bufs=1))
         shared = ctx.enter_context(tc.tile_pool(name="shared", bufs=1))
 
         def tile(shape, dtype, name):
@@ -56,14 +60,14 @@ def tile_picked_sortpair_relu_po_kernel(
         xw_table = tile_at(AT_WORDS, [P, T], U32, "xw_table")
         xw_picked = tile([P, S], U32, "xw_picked")
         w1_raw = tile([P, PACK, H], F32, "w1_raw")
-        w1_bf = tile_at(AT_W1, [P, PACK * H], BF16, "w1_bf")
-        w1_codes = tile([P, P], U32, "w1_codes")
-        w1_later = tile_at(AT_WORDS, [P, H - P], U32, "w1_later")
+        w1_bf = tile([P, PACK * H], BF16, "w1_bf")
+        w1_early = tile([P, 2 * P], U32, "w1_early")
+        w1_later = tile_at(AT_WORDS, [P, 2 * P], U32, "w1_later")
         w1_plane = tile([P, H], U8, "w1_plane")
         w2w_raw = tile_at(AT_SCALES, [P, 2 * N], U8, "w2w_raw")
         w2s_raw = tile([P, N], U8, "w2s_raw")
-        w2_codes = tile_at(AT_PARTS, [P, 2 * N], U8, "w2_codes")
-        w2_plane = tile_at(AT_W1, [P, N], U8, "w2_plane")
+        w2_codes = tile_at(AT_UP3, [P, 2 * N], U8, "w2_codes")
+        w2_plane = tile_at(AT_B3, [P, N], U8, "w2_plane")
 
         nc.gpsimd.memset(xs_table[:, :CLEARED].bitcast(I32), 0)
         nc.vector.memset(xs_plane[:].bitcast(I32), 0)
@@ -102,9 +106,10 @@ def tile_picked_sortpair_relu_po_kernel(
         nc.vector.tensor_copy(out=w1_dst, in_=w1_src)
 
         def w1_words(first, count):
-            if first == 0:
-                return w1_codes[:].bitcast(FP8X4)
-            return w1_later[:, P * (first - 1) : P * (first - 1 + count)].bitcast(FP8X4)
+            n = ORDER.index(first)
+            if n < 2:
+                return w1_early[:, P * n : P * (n + count)].bitcast(FP8X4)
+            return w1_later[:, P * (n - 2) : P * (n - 2 + count)].bitcast(FP8X4)
 
         def quantise_w1(first, count):
             nc.vector.quantize_mx(
@@ -113,18 +118,23 @@ def tile_picked_sortpair_relu_po_kernel(
                 in_=w1_bf[:, PACK * P * first : PACK * P * (first + count)],
             )
 
-        quantise_w1(0, 1)
+        quantise_w1(ORDER[0], 2)
 
-        y = [tile([P, S], F32, "y%d" % t) for t in range(PACK)]
+        y = [tile([P, S], F32, "y0")]
+        y = y + [tile_at(AT_Y2, [P, S], F32, "y1"), tile_at(AT_Y2, [P, S], F32, "y2"), tile_at(AT_Y3, [P, S], F32, "y3")]
+
+        def bank_tile(u):
+            return psum.tile([P, S], F32, name="bank%d" % u)
 
         def pick_words(cols):
             nc.vector.tensor_copy(
                 xw_picked[:, cols], xw_table[:].indirect(offs_sb[:, cols.start // 16 : cols.stop // 16])
             )
 
-        def first_product(t, cols):
+        def first_product(n, cols, u, on_vector=False):
+            t = ORDER[n]
             width = cols.stop - cols.start
-            bank = psum.tile([P, S], F32, name="bank")
+            bank = bank_tile(u)
             rows = slice(P * t, P * (t + 1))
             nc.tensor.matmul_mx(
                 out=bank[:, :width],
@@ -135,101 +145,85 @@ def tile_picked_sortpair_relu_po_kernel(
                 start=True,
                 stop=True,
             )
-            nc.scalar.activation(out=y[t][:, cols], in_=bank[:, :width], func=RELU)
+            if on_vector:
+                nc.vector.tensor_scalar_max(y[n][:, cols], bank[:, :width], 0.0)
+            else:
+                nc.scalar.activation(out=y[n][:, cols], in_=bank[:, :width], func=RELU)
 
         chunk = [slice(CHUNK * c, CHUNK * (c + 1)) for c in range(CHUNKS)]
         pick_words(slice(0, HALF))
-        first_product(0, slice(0, HALF))
+        first_product(0, slice(0, HALF), 0)
         pick_words(slice(HALF, S))
-        first_product(0, chunk[2])
-        first_product(0, chunk[3])
-        quantise_w1(1, 1)
-        quantise_w1(2, 2)
-        for t in range(1, PACK):
-            first_product(t, slice(0, S))
+        first_product(1, slice(0, HALF), 1, on_vector=True)
+        first_product(0, chunk[2], 2)
+        first_product(0, chunk[3], 3)
+        quantise_w1(ORDER[2], 1)
+        quantise_w1(ORDER[3], 1)
+
+        last = PACK - 1
+        a = [tile([P, V], F32, "a%d" % n) for n in range(PACK)]
+        b = [tile([P, V], F32, "b%d" % n) for n in range(last)]
+        b.append(tile_at(AT_B3, [P, V], F32, "b3"))
+        up = [tile_at(AT_UP0, [P, V], F32, "up0"), tile_at(AT_UP1, [P, V], F32, "up1")]
+        up = up + [tile([P, V], F32, "up2"), tile_at(AT_UP3, [P, V], F32, "up3")]
+        mn = [tile([P, V], F32, "mn%d" % n) for n in range(last)]
+        mn.append(tile_at(AT_UP1, [P, V], F32, "mn3"))
+        mx = [tile([P, V], F32, "mx0"), tile_at(AT_Y2, [P, V], F32, "mx1")]
+        mx = mx + [tile([P, V], F32, "mx2"), tile_at(AT_Z0, [P, V], F32, "mx3")]
+        z = [tile_at(AT_Z0, [P, S], F32, "z0"), tile_at(AT_UP0, [P, S], F32, "z1")]
+        z = z + [tile_at(AT_Y2, [P, S], F32, "z2"), tile([P, S], F32, "z3")]
+        z_bf = tile_at(AT_Y3 + 4 * V, [P, S, PACK], BF16, "z_bf")
+
+        def fetch(out, n, places):
+            nc.scalar.activation(out=out[n][:], in_=y[n][:].indirect(places[:]), func=COPY)
+
+        def smaller(n):
+            nc.vector.tensor_tensor(mn[n][:], a[n][:], b[n][:], ALU.min)
+
+        def larger(n):
+            nc.gpsimd.tensor_tensor(up[n][:], a[n][:], mn[n][:], ALU.subtract)
+            nc.gpsimd.tensor_tensor(mx[n][:], b[n][:], up[n][:], ALU.add)
+
+        def put_a(n):
+            nc.vector.tensor_copy(z[n][:].indirect(la_sb[:]), mn[n][:])
+
+        def put_b(n):
+            nc.vector.tensor_copy(z[n][:].indirect(lb_sb[:]), mx[n][:])
+
+        def round_z(copy, n, cols):
+            copy(out=z_bf[:, cols, ORDER[n]], in_=z[n][:, cols])
+
+        nc.vector.tensor_copy(a[0][:], y[0][:].indirect(la_sb[:]))
+        fetch(b, 0, lb_sb)
+        for n in range(1, PACK):
+            first_product(n, slice(HALF if n == 1 else 0, S), n + 2)
+            fetch(a, n, la_sb)
+            fetch(b, n, lb_sb)
+        smaller(0)
+        larger(0)
+        put_a(0)
+        smaller(1)
+        larger(1)
+        put_b(0)
+        put_a(1)
+        smaller(2)
+        larger(2)
+        put_b(1)
+        round_z(nc.scalar.copy, 0, slice(0, S))
+        smaller(3)
+        larger(3)
+        put_a(2)
+        put_a(3)
+        round_z(nc.scalar.copy, 1, slice(0, S))
+        put_b(2)
+        put_b(3)
+        for cols in (slice(0, HALF), slice(HALF, S)):
+            round_z(nc.scalar.copy, 2, cols)
 
         nc.gpsimd.tensor_copy(
             out=w2_plane[:].rearrange("p (t m) -> p t m", t=PACK),
             in_=w2s_raw[:].rearrange("p (m t) -> p t m", t=PACK),
         )
-
-        by_min = PACK - 1
-        by_masks = range(by_min)
-        last = by_min - 1
-        ab = [tile([P, 2, V], F32, "ab%d" % t) for t in range(PACK)]
-        a = [ab[t][:, 0, :] for t in range(PACK)]
-        b = [ab[t][:, 1, :] for t in range(PACK)]
-        up = [tile([P, V], F32, "up%d" % t) for t in range(2, PACK)]
-        up = [tile_at(AT_UP0, [P, V], F32, "up0"), tile_at(AT_UP1, [P, V], F32, "up1")] + up
-        mn = [tile([P, V], F32, "mn%d" % t) for t in by_masks]
-        mn.append(tile_at(AT_UP0 + 2 * V, [P, V], F32, "mn3"))
-        mx = [tile([P, V], F32, "mx%d" % t) for t in range(PACK)]
-        diff = [tile([P, V], F32, "diff%d" % t) for t in range(last)]
-        diff.append(tile_at(AT_UP0 - 2 * V, [P, V], F32, "diff2"))
-        take = [tile([P, 2, V], F32, "take%d" % t) for t in by_masks]
-        parts = [tile([P, 2, V], F32, "parts%d" % t) for t in range(last)]
-        parts.append(tile_at(AT_PARTS, [P, 2, V], F32, "parts2"))
-        z = [tile([P, S], F32, "z%d" % t) for t in by_masks]
-        z.append(tile_at(AT_UP1, [P, S], F32, "z3"))
-        z_bf = tile([P, S, PACK], BF16, "z_bf")
-
-        def fetch(t):
-            nc.vector.tensor_copy(a[t], y[t][:].indirect(la_sb[:]))
-            nc.vector.tensor_copy(b[t], y[t][:].indirect(lb_sb[:]))
-
-        def compare(t):
-            nc.gpsimd.tensor_tensor(diff[t][:], a[t], b[t], ALU.subtract)
-            nc.scalar.activation(out=up[t][:], in_=diff[t][:], func=RELU)
-            nc.scalar.activation(out=take[t][:, 1, :], in_=up[t][:], func=SIGN)
-            nc.scalar.activation(out=take[t][:, 0, :], in_=take[t][:, 1, :], func=RELU, scale=-1.0, bias=1.0)
-
-        def larger(t):
-            nc.gpsimd.tensor_tensor(mx[t][:], b[t], up[t][:], ALU.add)
-
-        def products(t):
-            nc.gpsimd.tensor_tensor(parts[t][:], ab[t][:], take[t][:], ALU.mult)
-
-        def smaller(t):
-            nc.gpsimd.tensor_tensor(mn[t][:], parts[t][:, 0, :], parts[t][:, 1, :], ALU.add)
-
-        def put_a(t):
-            nc.vector.tensor_copy(z[t][:].indirect(la_sb[:]), mn[t][:])
-
-        def put_b(t):
-            nc.vector.tensor_copy(z[t][:].indirect(lb_sb[:]), mx[t][:])
-
-        def round_z(copy, t, cols):
-            copy(out=z_bf[:, cols, t], in_=z[t][:, cols])
-
-        for t in range(PACK):
-            fetch(t)
-        compare(0)
-        compare(1)
-        larger(0)
-        put_b(0)
-        nc.vector.tensor_tensor(mn[by_min][:], a[by_min], b[by_min], ALU.min)
-        larger(1)
-        put_b(1)
-        put_a(by_min)
-        compare(2)
-        products(0)
-        larger(2)
-        put_b(2)
-        nc.gpsimd.tensor_tensor(up[by_min][:], a[by_min], mn[by_min][:], ALU.subtract)
-        smaller(0)
-        put_a(0)
-        larger(by_min)
-        put_b(by_min)
-        round_z(nc.scalar.copy, 0, slice(0, S))
-        nc.scalar.copy(out=z_bf[:, :, 2:4], in_=z[by_min][:].unsqueeze(2).to_broadcast([P, S, 2]))
-        for t in range(1, by_min):
-            products(t)
-        for t in range(1, by_min):
-            smaller(t)
-            put_a(t)
-        for cols in (slice(0, HALF), slice(HALF, S)):
-            round_z(nc.scalar.copy, 1, cols)
-
         nc.gpsimd.tensor_copy(
             out=w2_codes[:].rearrange("p (t m b) -> p t m b", t=PACK, b=2),
             in_=w2w_raw[:].rearrange("p (m t b) -> p t m b", t=PACK, b=2),
@@ -252,7 +246,7 @@ def tile_picked_sortpair_relu_po_kernel(
                 in_=z_bf[:, chunk[c], :].rearrange("p c t -> p (c t)"),
             )
             per_bank = 2
-            banks[c] = [psum.tile([P, S], F32, name="bank") for u in range(PACK // per_bank)]
+            banks[c] = [bank_tile(per_bank * c + u) for u in range(PACK // per_bank)]
             for t in range(PACK):
                 at = CHUNK * (t % per_bank)
                 nc.tensor.matmul_mx(

@@ -24,15 +24,14 @@ HALF = S // 2
 CHUNK = 128
 CHUNKS = S // CHUNK
 CLEARED = T // 2
-ORDER = (1, 2, 3, 0)
+ORDER = (0, 2, 3, 1)
 AT_Z0 = 0
-AT_UP0 = AT_Z0 + 4 * S
-AT_UP1 = AT_UP0 + 4 * S
-AT_Y2 = AT_UP1 + 4 * V
-AT_Y3 = AT_Y2 + 4 * V
-AT_UP3 = AT_Y3 + 4 * V + 2 * PACK * S
-AT_B3 = AT_UP3 + 4 * V
-AT_SCALES = AT_B3 + 4 * V
+AT_MX1 = AT_Z0 + 4 * S
+AT_Y3 = AT_MX1 + 4 * V
+AT_Y1 = AT_Y3 + 4 * V
+AT_RIGHT1 = AT_Y1 + 2 * PACK * S
+AT_B3 = AT_RIGHT1 + 8 * V
+AT_SCALES = AT_B3 + 6 * V
 AT_WORDS = AT_SCALES + T
 
 
@@ -61,12 +60,12 @@ def tile_picked_sortpair_relu_po_kernel(
         xw_picked = tile([P, S], U32, "xw_picked")
         w1_raw = tile([P, PACK, H], F32, "w1_raw")
         w1_bf = tile([P, PACK * H], BF16, "w1_bf")
-        w1_early = tile([P, 2 * P], U32, "w1_early")
-        w1_later = tile_at(AT_WORDS, [P, 2 * P], U32, "w1_later")
+        w1_codes = [tile([P, P], U32, "w1_codes%d" % n) for n in range(2)]
+        w1_codes = w1_codes + [tile_at(AT_WORDS + 4 * P * n, [P, P], U32, "w1_codes%d" % n) for n in range(2, PACK)]
         w1_plane = tile([P, H], U8, "w1_plane")
         w2w_raw = tile_at(AT_SCALES, [P, 2 * N], U8, "w2w_raw")
         w2s_raw = tile([P, N], U8, "w2s_raw")
-        w2_codes = tile_at(AT_UP3, [P, 2 * N], U8, "w2_codes")
+        w2_codes = tile_at(AT_RIGHT1, [P, 2 * N], U8, "w2_codes")
         w2_plane = tile_at(AT_B3, [P, N], U8, "w2_plane")
 
         nc.gpsimd.memset(xs_table[:, :CLEARED].bitcast(I32), 0)
@@ -105,23 +104,19 @@ def tile_picked_sortpair_relu_po_kernel(
         w1_src = w1_raw[:].rearrange("p j (m t) -> p m j t", t=PACK)
         nc.vector.tensor_copy(out=w1_dst, in_=w1_src)
 
-        def w1_words(first, count):
-            n = ORDER.index(first)
-            if n < 2:
-                return w1_early[:, P * n : P * (n + count)].bitcast(FP8X4)
-            return w1_later[:, P * (n - 2) : P * (n - 2 + count)].bitcast(FP8X4)
-
-        def quantise_w1(first, count):
+        def quantise_w1(n):
+            t = ORDER[n]
             nc.vector.quantize_mx(
-                out=w1_words(first, count),
-                scales=w1_plane[:, P * first : P * (first + count)],
-                in_=w1_bf[:, PACK * P * first : PACK * P * (first + count)],
+                out=w1_codes[n][:].bitcast(FP8X4),
+                scales=w1_plane[:, P * t : P * (t + 1)],
+                in_=w1_bf[:, PACK * P * t : PACK * P * (t + 1)],
             )
 
-        quantise_w1(ORDER[0], 2)
+        quantise_w1(0)
+        quantise_w1(1)
 
         y = [tile([P, S], F32, "y0")]
-        y = y + [tile_at(AT_Y2, [P, S], F32, "y1"), tile_at(AT_Y2, [P, S], F32, "y2"), tile_at(AT_Y3, [P, S], F32, "y3")]
+        y = y + [tile_at(AT_Y1, [P, S], F32, "y1"), tile_at(AT_Y1, [P, S], F32, "y2"), tile_at(AT_Y3, [P, S], F32, "y3")]
 
         def bank_tile(u):
             return psum.tile([P, S], F32, name="bank%d" % u)
@@ -138,7 +133,7 @@ def tile_picked_sortpair_relu_po_kernel(
             rows = slice(P * t, P * (t + 1))
             nc.tensor.matmul_mx(
                 out=bank[:, :width],
-                lhsT=w1_words(t, 1),
+                lhsT=w1_codes[n][:].bitcast(FP8X4),
                 lhsT_scale=w1_plane[:, rows],
                 rhs=xw_picked[:, cols].bitcast(FP8X4),
                 rhs_scale=xs_plane[:, cols],
@@ -153,47 +148,52 @@ def tile_picked_sortpair_relu_po_kernel(
         chunk = [slice(CHUNK * c, CHUNK * (c + 1)) for c in range(CHUNKS)]
         pick_words(slice(0, HALF))
         first_product(0, slice(0, HALF), 0)
+        first_product(1, slice(0, HALF), 1)
         pick_words(slice(HALF, S))
-        first_product(1, slice(0, HALF), 1, on_vector=True)
         first_product(0, chunk[2], 2)
         first_product(0, chunk[3], 3)
-        quantise_w1(ORDER[2], 1)
-        quantise_w1(ORDER[3], 1)
+        for n in range(2, PACK):
+            quantise_w1(n)
 
         last = PACK - 1
-        a = [tile([P, V], F32, "a%d" % n) for n in range(PACK)]
-        b = [tile([P, V], F32, "b%d" % n) for n in range(last)]
-        b.append(tile_at(AT_B3, [P, V], F32, "b3"))
-        up = [tile_at(AT_UP0, [P, V], F32, "up0"), tile_at(AT_UP1, [P, V], F32, "up1")]
-        up = up + [tile([P, V], F32, "up2"), tile_at(AT_UP3, [P, V], F32, "up3")]
-        mn = [tile([P, V], F32, "mn%d" % n) for n in range(last)]
-        mn.append(tile_at(AT_UP1, [P, V], F32, "mn3"))
-        mx = [tile([P, V], F32, "mx0"), tile_at(AT_Y2, [P, V], F32, "mx1")]
-        mx = mx + [tile([P, V], F32, "mx2"), tile_at(AT_Z0, [P, V], F32, "mx3")]
-        z = [tile_at(AT_Z0, [P, S], F32, "z0"), tile_at(AT_UP0, [P, S], F32, "z1")]
-        z = z + [tile_at(AT_Y2, [P, S], F32, "z2"), tile([P, S], F32, "z3")]
-        z_bf = tile_at(AT_Y3 + 4 * V, [P, S, PACK], BF16, "z_bf")
+        left = [tile([P, 2, V], F32, "left%d" % u) for u in range(2)]
+        right = [tile([P, 2, V], F32, "right0"), tile_at(AT_RIGHT1, [P, 2, V], F32, "right1")]
+        joint = [tile([P, 2, V], F32, "joint%d" % u) for u in range(2)]
+        a, b, mn, mx, down = [], [], [], [], []
+        for u in range(2):
+            a = a + [tile([P, V], F32, "a%d" % (2 * u))[:], right[u][:, 1, :]]
+            mn = mn + [tile([P, V], F32, "mn%d" % (2 * u))[:], left[u][:, 1, :]]
+            down = down + [right[u][:, 0, :], joint[u][:, 1, :]]
+        b = [left[0][:, 0, :], tile_at(AT_B3, [P, V], F32, "b1")[:], left[1][:, 0, :], tile_at(AT_B3 + 2 * V, [P, V], F32, "b3")[:]]
+        mx = [joint[0][:, 0, :], tile_at(AT_MX1, [P, V], F32, "mx1")[:]]
+        mx = mx + [joint[1][:, 0, :], tile_at(AT_Z0, [P, V], F32, "mx3")[:]]
+        z = [tile_at(AT_Z0, [P, S], F32, "z0"), tile([P, S], F32, "z1")]
+        z = z + [tile_at(AT_MX1, [P, S], F32, "z2"), tile([P, S], F32, "z3")]
+        z_bf = tile_at(AT_Y1, [P, S, PACK], BF16, "z_bf")
 
         def fetch(out, n, places):
-            nc.scalar.activation(out=out[n][:], in_=y[n][:].indirect(places[:]), func=COPY)
+            nc.scalar.activation(out=out[n], in_=y[n][:].indirect(places[:]), func=COPY)
 
         def smaller(n):
-            nc.vector.tensor_tensor(mn[n][:], a[n][:], b[n][:], ALU.min)
+            nc.vector.tensor_tensor(mn[n], a[n], b[n], ALU.min)
 
         def larger(n):
-            nc.gpsimd.tensor_tensor(up[n][:], a[n][:], mn[n][:], ALU.subtract)
-            nc.gpsimd.tensor_tensor(mx[n][:], b[n][:], up[n][:], ALU.add)
+            if n % 2 == 0:
+                nc.gpsimd.tensor_tensor(down[n], mn[n], a[n], ALU.subtract)
+            else:
+                nc.gpsimd.tensor_tensor(joint[n // 2][:], left[n // 2][:], right[n // 2][:], ALU.subtract)
+                nc.gpsimd.tensor_tensor(mx[n], b[n], down[n], ALU.subtract)
 
         def put_a(n):
-            nc.vector.tensor_copy(z[n][:].indirect(la_sb[:]), mn[n][:])
+            nc.vector.tensor_copy(z[n][:].indirect(la_sb[:]), mn[n])
 
         def put_b(n):
-            nc.vector.tensor_copy(z[n][:].indirect(lb_sb[:]), mx[n][:])
+            nc.vector.tensor_copy(z[n][:].indirect(lb_sb[:]), mx[n])
 
         def round_z(copy, n, cols):
             copy(out=z_bf[:, cols, ORDER[n]], in_=z[n][:, cols])
 
-        nc.vector.tensor_copy(a[0][:], y[0][:].indirect(la_sb[:]))
+        nc.vector.tensor_copy(a[0], y[0][:].indirect(la_sb[:]))
         fetch(b, 0, lb_sb)
         for n in range(1, PACK):
             first_product(n, slice(HALF if n == 1 else 0, S), n + 2)
@@ -204,8 +204,12 @@ def tile_picked_sortpair_relu_po_kernel(
         put_a(0)
         smaller(1)
         larger(1)
-        put_b(0)
+        nc.gpsimd.tensor_copy(
+            out=w2_plane[:].rearrange("p (t m) -> p t m", t=PACK),
+            in_=w2s_raw[:].rearrange("p (m t) -> p t m", t=PACK),
+        )
         put_a(1)
+        put_b(0)
         smaller(2)
         larger(2)
         put_b(1)
@@ -220,10 +224,6 @@ def tile_picked_sortpair_relu_po_kernel(
         for cols in (slice(0, HALF), slice(HALF, S)):
             round_z(nc.scalar.copy, 2, cols)
 
-        nc.gpsimd.tensor_copy(
-            out=w2_plane[:].rearrange("p (t m) -> p t m", t=PACK),
-            in_=w2s_raw[:].rearrange("p (m t) -> p t m", t=PACK),
-        )
         nc.gpsimd.tensor_copy(
             out=w2_codes[:].rearrange("p (t m b) -> p t m b", t=PACK, b=2),
             in_=w2w_raw[:].rearrange("p (m t b) -> p t m b", t=PACK, b=2),

@@ -26,7 +26,8 @@ CHUNKS = S // CHUNK
 CLEARED = T // 2
 ORDER = (0, 2, 3, 1)
 AT_Z0 = 0
-AT_MX1 = AT_Z0 + 4 * S
+AT_Z1 = AT_Z0 + 4 * S
+AT_MX1 = AT_Z1 + 4 * S
 AT_Y3 = AT_MX1 + 4 * V
 AT_Y1 = AT_Y3 + 4 * V
 AT_RIGHT1 = AT_Y1 + 2 * PACK * S
@@ -166,8 +167,8 @@ def tile_picked_sortpair_relu_po_kernel(
             down = down + [right[u][:, 0, :], joint[u][:, 1, :]]
         b = [left[0][:, 0, :], tile_at(AT_B3, [P, V], F32, "b1")[:], left[1][:, 0, :], tile_at(AT_B3 + 2 * V, [P, V], F32, "b3")[:]]
         mx = [joint[0][:, 0, :], tile_at(AT_MX1, [P, V], F32, "mx1")[:]]
-        mx = mx + [joint[1][:, 0, :], tile_at(AT_Z0, [P, V], F32, "mx3")[:]]
-        z = [tile_at(AT_Z0, [P, S], F32, "z0"), tile([P, S], F32, "z1")]
+        mx = mx + [joint[1][:, 0, :], tile_at(AT_Z1 - 2 * V, [P, V], F32, "mx3")[:]]
+        z = [tile_at(AT_Z0, [P, S], F32, "z0"), tile_at(AT_Z1, [P, S], F32, "z1")]
         z = z + [tile_at(AT_MX1, [P, S], F32, "z2"), tile([P, S], F32, "z3")]
         z_bf = tile_at(AT_Y1, [P, S, PACK], BF16, "z_bf")
 
@@ -221,8 +222,8 @@ def tile_picked_sortpair_relu_po_kernel(
         round_z(nc.scalar.copy, 1, slice(0, S))
         put_b(2)
         put_b(3)
-        for cols in (slice(0, HALF), slice(HALF, S)):
-            round_z(nc.scalar.copy, 2, cols)
+        round_z(nc.scalar.copy, 2, slice(0, HALF))
+        nc.gpsimd.tensor_scalar(z_bf[:, HALF:, ORDER[2]], z[2][:, HALF:], 1.0, 0.0, ALU.mult, ALU.add)
 
         nc.gpsimd.tensor_copy(
             out=w2_codes[:].rearrange("p (t m b) -> p t m b", t=PACK, b=2),
@@ -284,7 +285,7 @@ def tile_picked_sortpair_relu_po_kernel(
             nc.sync.dma_start(out=words_dst[:, cols], in_=o_codes[:, cols].bitcast(I32))
 
         for c in range(CHUNKS):
-            round_z(nc.scalar.copy if c % 2 else nc.vector.tensor_copy, last, chunk[c])
+            round_z(nc.vector.tensor_copy if c == 1 else nc.scalar.copy, last, chunk[c])
         for c in range(CHUNKS):
             second_product(c)
         leave_half(0, 0, nc.scalar.copy)

@@ -66,7 +66,7 @@ def tile_picked_sortpair_relu_po_kernel(
         w1_plane = tile([P, H], U8, "w1_plane")
         w2w_raw = tile_at(AT_SCALES, [P, 2 * N], U8, "w2w_raw")
         w2s_raw = tile([P, N], U8, "w2s_raw")
-        w2_codes = tile_at(AT_RIGHT1, [P, 2 * N], U8, "w2_codes")
+        w2_codes = tile_at(AT_Z1 + 4 * V, [P, 2 * N], U8, "w2_codes")
         w2_plane = tile_at(AT_B3, [P, N], U8, "w2_plane")
 
         nc.gpsimd.memset(xs_table[:, :CLEARED].bitcast(I32), 0)
@@ -220,15 +220,15 @@ def tile_picked_sortpair_relu_po_kernel(
         put_a(2)
         put_a(3)
         round_z(nc.scalar.copy, 1, slice(0, S))
+        nc.scalar.copy(
+            out=w2_codes[:].bitcast(U16).rearrange("p (t m) -> p t m", t=PACK),
+            in_=w2w_raw[:].bitcast(U16).rearrange("p (m t) -> p t m", t=PACK),
+        )
         put_b(2)
         put_b(3)
-        round_z(nc.scalar.copy, 2, slice(0, HALF))
-        nc.gpsimd.tensor_scalar(z_bf[:, HALF:, ORDER[2]], z[2][:, HALF:], 1.0, 0.0, ALU.mult, ALU.add)
+        round_z(nc.scalar.copy, 2, slice(0, 3 * CHUNK))
+        nc.gpsimd.tensor_scalar(z_bf[:, chunk[3], ORDER[2]], z[2][:, chunk[3]], 1.0, 0.0, ALU.mult, ALU.add)
 
-        nc.gpsimd.tensor_copy(
-            out=w2_codes[:].rearrange("p (t m b) -> p t m b", t=PACK, b=2),
-            in_=w2w_raw[:].rearrange("p (m t b) -> p t m b", t=PACK, b=2),
-        )
 
         z_codes = tile([P, S], U32, "z_codes")
         z_plane = tile([P, S], U8, "z_plane")

@@ -67,7 +67,7 @@ def tile_picked_sortpair_relu_po_kernel(
         w2w_raw = tile_at(AT_SCALES, [P, 2 * N], U8, "w2w_raw")
         w2s_raw = tile([P, N], U8, "w2s_raw")
         w2_codes = tile_at(AT_Z1 + 4 * V, [P, 2 * N], U8, "w2_codes")
-        w2_plane = tile_at(AT_B3, [P, N], U8, "w2_plane")
+        w2_plane = [tile_at(at, [P, N // 2], U8, "w2_plane%d" % u) for u, at in enumerate((AT_B3, AT_RIGHT1))]
 
         nc.gpsimd.memset(xs_table[:, :CLEARED].bitcast(I32), 0)
         nc.vector.memset(xs_plane[:].bitcast(I32), 0)
@@ -191,6 +191,12 @@ def tile_picked_sortpair_relu_po_kernel(
         def put_b(n):
             nc.vector.tensor_copy(z[n][:].indirect(lb_sb[:]), mx[n])
 
+        def deal_plane(u):
+            nc.gpsimd.tensor_copy(
+                out=w2_plane[u][:].rearrange("p (t m) -> p t m", t=2),
+                in_=w2s_raw[:].rearrange("p (m t) -> p t m", t=PACK)[:, 2 * u : 2 * u + 2, :],
+            )
+
         def round_z(copy, n, cols):
             copy(out=z_bf[:, cols, ORDER[n]], in_=z[n][:, cols])
 
@@ -205,10 +211,7 @@ def tile_picked_sortpair_relu_po_kernel(
         put_a(0)
         smaller(1)
         larger(1)
-        nc.gpsimd.tensor_copy(
-            out=w2_plane[:].rearrange("p (t m) -> p t m", t=PACK),
-            in_=w2s_raw[:].rearrange("p (m t) -> p t m", t=PACK),
-        )
+        deal_plane(0)
         put_a(1)
         put_b(0)
         smaller(2)
@@ -217,6 +220,7 @@ def tile_picked_sortpair_relu_po_kernel(
         round_z(nc.scalar.copy, 0, slice(0, S))
         smaller(3)
         larger(3)
+        deal_plane(1)
         put_a(2)
         put_a(3)
         round_z(nc.scalar.copy, 1, slice(0, S))
@@ -253,7 +257,7 @@ def tile_picked_sortpair_relu_po_kernel(
                 nc.tensor.matmul_mx(
                     out=banks[c][t // per_bank][:, at : at + CHUNK],
                     lhsT=w2_codes[:, 2 * P * t : 2 * P * (t + 1)].bitcast(FP4X4),
-                    lhsT_scale=w2_plane[:, P * t : P * (t + 1)],
+                    lhsT_scale=w2_plane[t // 2][:, P * (t % 2) : P * (t % 2 + 1)],
                     rhs=z_codes[:, chunk[c]].bitcast(FP8X4),
                     rhs_scale=z_plane[:, chunk[c]],
                     start=True,

@@ -240,76 +240,99 @@ def tile_picked_sortpair_relu_po_kernel(
         o_plane = tile([P, S], U8, "o_plane")
         out_rows = out_0.rearrange("(p t) c -> p t c", t=PACK)
         words_dst = out_1[0].rearrange("p c r -> p (c r)").bitcast(I32)
+        widths = (128, 128, 128, 128)
+        starts = [sum(widths[:g]) for g in range(len(widths))]
+        group = [slice(starts[g], starts[g] + widths[g]) for g in range(len(widths))]
+        per_bank = [2 * CHUNK // w for w in widths]
+        first_bank = [sum(PACK // n for n in per_bank[:g]) for g in range(len(widths))]
         banks = {}
-        o_f32 = [tile([P, PACK, CHUNK], F32, "o_f32_%d" % c) for c in range(CHUNKS)]
-        o_bf = [tile([P, CHUNK, PACK], BF16, "o_bf_%d" % c) for c in range(CHUNKS)]
+        o_f32 = [tile([P, PACK, widths[g]], F32, "o_f32_%d" % g) for g in range(len(widths))]
+        o_bf = [tile([P, widths[g], PACK], BF16, "o_bf_%d" % g) for g in range(len(widths))]
 
-        def second_product(c):
+        def second_product(g):
             nc.vector.quantize_mx(
-                out=z_codes[:, chunk[c]].bitcast(FP8X4),
-                scales=z_plane[:, chunk[c]],
-                in_=z_bf[:, chunk[c], :].rearrange("p c t -> p (c t)"),
+                out=z_codes[:, group[g]].bitcast(FP8X4),
+                scales=z_plane[:, group[g]],
+                in_=z_bf[:, group[g], :].rearrange("p c t -> p (c t)"),
             )
-            per_bank = 2
-            banks[c] = [bank_tile(per_bank * c + u) for u in range(PACK // per_bank)]
+            banks[g] = [bank_tile(first_bank[g] + u) for u in range(PACK // per_bank[g])]
             for t in range(PACK):
-                at = CHUNK * (t % per_bank)
+                at = widths[g] * (t % per_bank[g])
                 nc.tensor.matmul_mx(
-                    out=banks[c][t // per_bank][:, at : at + CHUNK],
+                    out=banks[g][t // per_bank[g]][:, at : at + widths[g]],
                     lhsT=w2_codes[:, 2 * P * t : 2 * P * (t + 1)].bitcast(FP4X4),
                     lhsT_scale=w2_plane[t // 2][:, P * (t % 2) : P * (t % 2 + 1)],
-                    rhs=z_codes[:, chunk[c]].bitcast(FP8X4),
-                    rhs_scale=z_plane[:, chunk[c]],
+                    rhs=z_codes[:, group[g]].bitcast(FP8X4),
+                    rhs_scale=z_plane[:, group[g]],
                     start=True,
                     stop=True,
                 )
 
-        def leave_half(c, u, copy):
-            rows = slice(2 * u, 2 * u + 2)
-            copy(out=o_f32[c][:, rows, :].rearrange("p t c -> p (t c)"), in_=banks[c][u][:, : 2 * CHUNK])
+        def leave(g, u, copy):
+            rows = slice(per_bank[g] * u, per_bank[g] * (u + 1))
+            copy(out=o_f32[g][:, rows, :].rearrange("p t c -> p (t c)"), in_=banks[g][u][:, : 2 * CHUNK])
 
-        def store_half(c, u):
-            rows = slice(2 * u, 2 * u + 2)
-            nc.sync.dma_start(out=out_rows[:, rows, chunk[c]], in_=o_f32[c][:, rows, :])
+        def store(g, rows, queue):
+            queue.dma_start(out=out_rows[:, rows, group[g]], in_=o_f32[g][:, rows, :])
 
-        def weave_from_sbuf(c):
+        def weave(g, cols):
             nc.vector.tensor_copy(
-                out=o_bf[c][:].rearrange("p (g i) t -> p g t i", i=4),
-                in_=o_f32[c][:].rearrange("p t (g i) -> p g t i", i=4),
+                out=o_bf[g][:, cols, :].rearrange("p (g i) t -> p g t i", i=4),
+                in_=o_f32[g][:, :, cols].rearrange("p t (g i) -> p g t i", i=4),
             )
 
-        def leave_codes(c):
+        def weave_pair(g, u, from_bank):
+            src = banks[g][u][:, : 2 * CHUNK].rearrange("p (t c) -> p c t", t=2)
+            if not from_bank:
+                src = o_f32[g][:, 2 * u : 2 * u + 2, :].rearrange("p t c -> p c t")
+            nc.vector.tensor_copy(out=o_bf[g][:, :, 2 * u : 2 * u + 2], in_=src)
+
+        def leave_codes(g, cols):
+            dst = slice(starts[g] + cols.start, starts[g] + cols.stop)
             nc.vector.quantize_mx(
-                out=o_codes[:, chunk[c]].bitcast(FP8X4),
-                scales=o_plane[:, chunk[c]],
-                in_=o_bf[c][:].rearrange("p c t -> p (c t)"),
+                out=o_codes[:, dst].bitcast(FP8X4),
+                scales=o_plane[:, dst],
+                in_=o_bf[g][:, cols, :].rearrange("p c t -> p (c t)"),
             )
 
-        def store_words(cols):
-            nc.sync.dma_start(out=words_dst[:, cols], in_=o_codes[:, cols].bitcast(I32))
+        def store_words(cols, queue):
+            queue.dma_start(out=words_dst[:, cols], in_=o_codes[:, cols].bitcast(I32))
 
-        for c in range(CHUNKS):
-            round_z(nc.vector.tensor_copy if c == 1 else nc.scalar.copy, last, chunk[c])
-        for c in range(CHUNKS):
-            second_product(c)
-        leave_half(0, 0, nc.scalar.copy)
-        store_half(0, 0)
-        leave_half(0, 1, nc.vector.tensor_copy)
-        store_half(0, 1)
-        weave_from_sbuf(0)
-        for c in range(1, CHUNKS):
-            for u in range(2):
-                leave_half(c, u, nc.scalar.copy)
-            queue = nc.scalar if c == CHUNKS - 1 else nc.sync
-            queue.dma_start(out=out_rows[:, :, chunk[c]], in_=o_f32[c][:])
-            weave_from_sbuf(c)
-            leave_codes(c - 1)
-            if c == 2:
-                store_words(slice(0, HALF))
-        leave_codes(CHUNKS - 1)
-        store_words(slice(HALF, S))
-        for q in range(QUADS):
-            queue = nc.scalar if q % 2 else nc.sync
+        def store_scales(q, queue):
             queue.dma_start(
                 out=out_2[0][4 * q : 4 * q + 4, :].bitcast(I32), in_=o_plane[32 * q : 32 * q + 4, :].bitcast(I32)
             )
+
+        by_scalar, by_vector = nc.scalar.copy, nc.vector.tensor_copy
+        narrow, wide, upper = slice(0, CHUNK), slice(0, 2 * CHUNK), slice(CHUNK, 2 * CHUNK)
+        for c in range(CHUNKS):
+            round_z(by_vector if c == 1 else by_scalar, last, chunk[c])
+        for g in range(len(widths)):
+            second_product(g)
+        leave(0, 0, by_scalar)
+        store(0, slice(0, 2), nc.sync)
+        leave(0, 1, by_scalar)
+        store(0, slice(2, 4), nc.sync)
+        leave(1, 0, by_vector)
+        weave(0, narrow)
+        leave(1, 1, by_scalar)
+        store(1, slice(0, 4), nc.sync)
+        weave(1, narrow)
+        leave_codes(0, narrow)
+        leave(2, 0, by_scalar)
+        leave(2, 1, by_scalar)
+        store(2, slice(0, 4), nc.sync)
+        weave(2, narrow)
+        leave_codes(1, narrow)
+        store_words(wide, nc.sync)
+        leave(3, 0, by_scalar)
+        leave(3, 1, by_scalar)
+        store(3, slice(0, 4), nc.scalar)
+        weave(3, narrow)
+        leave_codes(2, narrow)
+        leave_codes(3, narrow)
+        store_words(slice(HALF, S), nc.sync)
+        store_scales(0, nc.sync)
+        store_scales(1, nc.scalar)
+        store_scales(2, nc.sync)
+        store_scales(3, nc.scalar)

@@ -23,7 +23,8 @@ QUADS = 4
 HALF = S // 2
 CHUNK = 128
 CHUNKS = S // CHUNK
-CLEARED = T // 2
+CLEARED = 3 * T // 4
+AHEAD = 5 * H // 4
 ORDER = (0, 2, 3, 1)
 AT_Z0 = 0
 AT_Z1 = AT_Z0 + 4 * S
@@ -79,10 +80,12 @@ def tile_picked_sortpair_relu_po_kernel(
             out=xs_table[:, CLEARED:].bitcast(I32),
             in_=xs_rows[:, CLEARED // 4 :].unsqueeze(1).to_broadcast([16, 8, (T - CLEARED) // 4]),
         )
-        nc.sync.dma_start(out=w1_raw[:, :1], in_=w1_rows[:, :1])
+        w1_flat = w1_rows.rearrange("p j c -> p (j c)")
+        raw_flat = w1_raw[:].rearrange("p j c -> p (j c)")
+        nc.sync.dma_start(out=raw_flat[:, :AHEAD], in_=w1_flat[:, :AHEAD])
         nc.sync.dma_start(offs_sb[:], offs)
         nc.sync.dma_start(out=xs_table[0:P:8, :CLEARED].bitcast(I32), in_=xs_rows[:, : CLEARED // 4])
-        nc.sync.dma_start(out=w1_raw[:, 1:], in_=w1_rows[:, 1:])
+        nc.sync.dma_start(out=raw_flat[:, AHEAD:], in_=w1_flat[:, AHEAD:])
         nc.sync.dma_start(
             out=xw_table[:].bitcast(I32), in_=x_words[0].rearrange("p c r -> p (c r)").bitcast(I32)
         )

from contextlib import ExitStack

import concourse.mybir as mybir

K, T, S, V, N, H = 512, 2048, 512, 256, 512, 512
FLOPS = 2 * K * H * S + 2 * H * N * S

F32 = mybir.dt.float32
BF16 = mybir.dt.bfloat16
I32 = mybir.dt.int32
U32 = mybir.dt.uint32
U16 = mybir.dt.uint16
U8 = mybir.dt.uint8
FP8X4 = mybir.dt.float8_e4m3fn_x4
FP4X4 = mybir.dt.float4_e2m1fn_x4
ALU = mybir.AluOpType
RELU = mybir.ActivationFunctionType.Relu
COPY = mybir.ActivationFunctionType.Copy

P = 128
PACK = 4
QUADS = 4
HALF = S // 2
CHUNK = 128
CHUNKS = S // CHUNK
CLEARED = 3 * T // 4
AHEAD = 5 * H // 4
ORDER = (0, 2, 3, 1)
AT_Z0 = 0
AT_Z1 = AT_Z0 + 4 * S
AT_MX1 = AT_Z1 + 4 * S
AT_Y3 = AT_MX1 + 4 * V
AT_Y1 = AT_Y3 + 4 * V
AT_RIGHT1 = AT_Y1 + 2 * PACK * S
AT_B3 = AT_RIGHT1 + 8 * V
AT_SCALES = AT_B3 + 6 * V
AT_WORDS = AT_SCALES + T


def tile_picked_sortpair_relu_po_kernel(
    tc, x_words, x_scales, w1, w2_words, w2_scales, offs, la, lb, out_0, out_1, out_2
):
    nc = tc.nc
    with ExitStack() as ctx:
        keep = ctx.enter_context(tc.tile_pool(name="keep", bufs=1))
        psum = ctx.enter_context(tc.psum_pool(name="psum", bufs=1))
        shared = ctx.enter_context(tc.tile_pool(name="shared", bufs=1))

        def tile(shape, dtype, name):
            return keep.tile(shape, dtype, name=name, align_bytes=64)

        def tile_at(offset, shape, dtype, name):
            return shared.tile(shape, dtype, name=name, align_bytes=64, offset=offset)

        offs_sb = tile([P, S // 16], U16, "offs_sb")
        la_sb = tile([P, V // 16], U16, "la_sb")
        lb_sb = tile([P, V // 16], U16, "lb_sb")
        xs_table = tile_at(AT_SCALES, [P, T], U8, "xs_table")
        xs_picked = tile([P, S], U8, "xs_picked")
        xs_plane = tile([P, S], U8, "xs_plane")
        xw_table = tile_at(AT_WORDS, [P, T], U32, "xw_table")
        xw_picked = tile([P, S], U32, "xw_picked")
        w1_raw = tile([P, PACK, H], F32, "w1_raw")
        w1_bf = tile([P, PACK * H], BF16, "w1_bf")
        w1_codes = [tile([P, P], U32, "w1_codes%d" % n) for n in range(2)]
        w1_codes = w1_codes + [tile_at(AT_WORDS + 4 * P * n, [P, P], U32, "w1_codes%d" % n) for n in range(2, PACK)]
        w1_plane = tile([P, H], U8, "w1_plane")
        w2w_raw = tile_at(AT_SCALES, [P, 2 * N], U8, "w2w_raw")
        w2s_raw = tile([P, N], U8, "w2s_raw")
        w2_codes = tile_at(AT_Z1 + 4 * V, [P, 2 * N], U8, "w2_codes")
        w2_plane = [tile_at(at, [P, N // 2], U8, "w2_plane%d" % u) for u, at in enumerate((AT_B3, AT_RIGHT1))]

        nc.gpsimd.memset(xs_table[:, :CLEARED].bitcast(I32), 0)
        nc.vector.memset(xs_plane[:].bitcast(I32), 0)
        nc.gpsimd.memset(w2s_raw[:].bitcast(I32), 0)

        xs_rows = x_scales[0].bitcast(I32)
        w1_rows = w1.rearrange("(p j) c -> p j c", j=PACK)
        nc.sync.dma_start(
            out=xs_table[:, CLEARED:].bitcast(I32),
            in_=xs_rows[:, CLEARED // 4 :].unsqueeze(1).to_broadcast([16, 8, (T - CLEARED) // 4]),
        )
        w1_flat = w1_rows.rearrange("p j c -> p (j c)")
        raw_flat = w1_raw[:].rearrange("p j c -> p (j c)")
        nc.sync.dma_start(out=raw_flat[:, :AHEAD], in_=w1_flat[:, :AHEAD])
        nc.sync.dma_start(offs_sb[:], offs)
        nc.sync.dma_start(out=xs_table[0:P:8, :CLEARED].bitcast(I32), in_=xs_rows[:, : CLEARED // 4])
        nc.sync.dma_start(out=raw_flat[:, AHEAD:], in_=w1_flat[:, AHEAD:])
        nc.sync.dma_start(
            out=xw_table[:].bitcast(I32), in_=x_words[0].rearrange("p c r -> p (c r)").bitcast(I32)
        )
        nc.sync.dma_start(la_sb[:], la)
        nc.sync.dma_start(lb_sb[:], lb)
        for q in range(QUADS):
            nc.gpsimd.dma_start(
                out=w2s_raw[32 * q : 32 * q + 4, :].bitcast(I32), in_=w2_scales[0][4 * q : 4 * q + 4, :].bitcast(I32)
            )

        nc.vector.tensor_copy(xs_picked[:], xs_table[:].indirect(offs_sb[:]))
        for q in range(QUADS):
            nc.scalar.dma_start(
                out=xs_plane[32 * q : 32 * q + 4, :].bitcast(I32),
                in_=xs_picked[32 * q : 32 * q + 32 : 8, :].bitcast(I32),
            )
        nc.sync.dma_start(out=w2w_raw[:].bitcast(I32), in_=w2_words[0].bitcast(I32))

        w1_dst = w1_bf[:].rearrange("p (t m j) -> p m j t", t=PACK, j=PACK)
        w1_src = w1_raw[:].rearrange("p j (m t) -> p m j t", t=PACK)
        nc.vector.tensor_copy(out=w1_dst, in_=w1_src)

        def quantise_w1(n):
            t = ORDER[n]
            nc.vector.quantize_mx(
                out=w1_codes[n][:].bitcast(FP8X4),
                scales=w1_plane[:, P * t : P * (t + 1)],
                in_=w1_bf[:, PACK * P * t : PACK * P * (t + 1)],
            )

        quantise_w1(0)
        quantise_w1(1)

        y = [tile([P, S], F32, "y0")]
        y = y + [tile_at(AT_Y1, [P, S], F32, "y1"), tile_at(AT_Y1, [P, S], F32, "y2"), tile_at(AT_Y3, [P, S], F32, "y3")]

        def bank_tile(u):
            return psum.tile([P, S], F32, name="bank%d" % u)

        def pick_words(cols):
            nc.vector.tensor_copy(
                xw_picked[:, cols], xw_table[:].indirect(offs_sb[:, cols.start // 16 : cols.stop // 16])
            )

        def first_product(n, cols, u, on_vector=False):
            t = ORDER[n]
            width = cols.stop - cols.start
            bank = bank_tile(u)
            rows = slice(P * t, P * (t + 1))
            nc.tensor.matmul_mx(
                out=bank[:, :width],
                lhsT=w1_codes[n][:].bitcast(FP8X4),
                lhsT_scale=w1_plane[:, rows],
                rhs=xw_picked[:, cols].bitcast(FP8X4),
                rhs_scale=xs_plane[:, cols],
                start=True,
                stop=True,
            )
            if on_vector:
                nc.vector.tensor_scalar_max(y[n][:, cols], bank[:, :width], 0.0)
            else:
                nc.scalar.activation(out=y[n][:, cols], in_=bank[:, :width], func=RELU)

        chunk = [slice(CHUNK * c, CHUNK * (c + 1)) for c in range(CHUNKS)]
        pick_words(slice(0, HALF))
        first_product(0, slice(0, HALF), 0)
        first_product(1, slice(0, HALF), 1)
        pick_words(slice(HALF, S))
        first_product(0, chunk[2], 2)
        first_product(0, chunk[3], 3)
        for n in range(2, PACK):
            quantise_w1(n)

        last = PACK - 1
        left = [tile([P, 2, V], F32, "left%d" % u) for u in range(2)]
        right = [tile([P, 2, V], F32, "right0"), tile_at(AT_RIGHT1, [P, 2, V], F32, "right1")]
        joint = [tile([P, 2, V], F32, "joint%d" % u) for u in range(2)]
        a, b, mn, mx, down = [], [], [], [], []
        for u in range(2):
            a = a + [tile([P, V], F32, "a%d" % (2 * u))[:], right[u][:, 1, :]]
            mn = mn + [tile([P, V], F32, "mn%d" % (2 * u))[:], left[u][:, 1, :]]
            down = down + [right[u][:, 0, :], joint[u][:, 1, :]]
        b = [left[0][:, 0, :], tile_at(AT_B3, [P, V], F32, "b1")[:], left[1][:, 0, :], tile_at(AT_B3 + 2 * V, [P, V], F32, "b3")[:]]
        mx = [joint[0][:, 0, :], tile_at(AT_MX1, [P, V], F32, "mx1")[:]]
        mx = mx + [joint[1][:, 0, :], tile_at(AT_Z1 - 2 * V, [P, V], F32, "mx3")[:]]
        z = [tile_at(AT_Z0, [P, S], F32, "z0"), tile_at(AT_Z1, [P, S], F32, "z1")]
        z = z + [tile_at(AT_MX1, [P, S], F32, "z2"), tile([P, S], F32, "z3")]
        z_bf = tile_at(AT_Y1, [P, S, PACK], BF16, "z_bf")

        def fetch(out, n, places):
            nc.scalar.activation(out=out[n], in_=y[n][:].indirect(places[:]), func=COPY)

        def smaller(n):
            nc.vector.tensor_tensor(mn[n], a[n], b[n], ALU.min)

        def larger(n):
            if n % 2 == 0:
                nc.gpsimd.tensor_tensor(down[n], mn[n], a[n], ALU.subtract)
            else:
                nc.gpsimd.tensor_tensor(joint[n // 2][:], left[n // 2][:], right[n // 2][:], ALU.subtract)
                nc.gpsimd.tensor_tensor(mx[n], b[n], down[n], ALU.subtract)

        def put_a(n):
            nc.vector.tensor_copy(z[n][:].indirect(la_sb[:]), mn[n])

        def put_b(n):
            nc.vector.tensor_copy(z[n][:].indirect(lb_sb[:]), mx[n])

        def deal_plane(u):
            nc.gpsimd.tensor_copy(
                out=w2_plane[u][:].rearrange("p (t m) -> p t m", t=2),
                in_=w2s_raw[:].rearrange("p (m t) -> p t m", t=PACK)[:, 2 * u : 2 * u + 2, :],
            )

        def round_z(copy, n, cols):
            copy(out=z_bf[:, cols, ORDER[n]], in_=z[n][:, cols])

        nc.vector.tensor_copy(a[0], y[0][:].indirect(la_sb[:]))
        fetch(b, 0, lb_sb)
        for n in range(1, PACK):
            first_product(n, slice(HALF if n == 1 else 0, S), n + 2)
            fetch(a, n, la_sb)
            fetch(b, n, lb_sb)
        smaller(0)
        larger(0)
        put_a(0)
        smaller(1)
        larger(1)
        deal_plane(0)
        put_a(1)
        put_b(0)
        smaller(2)
        larger(2)
        put_b(1)
        round_z(nc.scalar.copy, 0, slice(0, S))
        smaller(3)
        larger(3)
        deal_plane(1)
        put_a(2)
        put_a(3)
        round_z(nc.scalar.copy, 1, slice(0, S))
        nc.scalar.copy(
            out=w2_codes[:].bitcast(U16).rearrange("p (t m) -> p t m", t=PACK),
            in_=w2w_raw[:].bitcast(U16).rearrange("p (m t) -> p t m", t=PACK),
        )
        put_b(2)
        put_b(3)
        round_z(nc.scalar.copy, 2, slice(0, 3 * CHUNK))
        nc.gpsimd.tensor_scalar(z_bf[:, chunk[3], ORDER[2]], z[2][:, chunk[3]], 1.0, 0.0, ALU.mult, ALU.add)


        z_codes = tile([P, S], U32, "z_codes")
        z_plane = tile([P, S], U8, "z_plane")
        o_codes = tile([P, S], U32, "o_codes")
        o_plane = tile([P, S], U8, "o_plane")
        out_rows = out_0.rearrange("(p t) c -> p t c", t=PACK)
        words_dst = out_1[0].rearrange("p c r -> p (c r)").bitcast(I32)
        widths = (128, 128, 128, 128)
        starts = [sum(widths[:g]) for g in range(len(widths))]
        group = [slice(starts[g], starts[g] + widths[g]) for g in range(len(widths))]
        per_bank = [2 * CHUNK // w for w in widths]
        first_bank = [sum(PACK // n for n in per_bank[:g]) for g in range(len(widths))]
        banks = {}
        o_f32 = [tile([P, PACK, widths[g]], F32, "o_f32_%d" % g) for g in range(len(widths))]
        o_bf = [tile([P, widths[g], PACK], BF16, "o_bf_%d" % g) for g in range(len(widths))]

        def second_product(g):
            nc.vector.quantize_mx(
                out=z_codes[:, group[g]].bitcast(FP8X4),
                scales=z_plane[:, group[g]],
                in_=z_bf[:, group[g], :].rearrange("p c t -> p (c t)"),
            )
            banks[g] = [bank_tile(first_bank[g] + u) for u in range(PACK // per_bank[g])]
            for t in range(PACK):
                at = widths[g] * (t % per_bank[g])
                nc.tensor.matmul_mx(
                    out=banks[g][t // per_bank[g]][:, at : at + widths[g]],
                    lhsT=w2_codes[:, 2 * P * t : 2 * P * (t + 1)].bitcast(FP4X4),
                    lhsT_scale=w2_plane[t // 2][:, P * (t % 2) : P * (t % 2 + 1)],
                    rhs=z_codes[:, group[g]].bitcast(FP8X4),
                    rhs_scale=z_plane[:, group[g]],
                    start=True,
                    stop=True,
                )

        def leave(g, u, copy):
            rows = slice(per_bank[g] * u, per_bank[g] * (u + 1))
            copy(out=o_f32[g][:, rows, :].rearrange("p t c -> p (t c)"), in_=banks[g][u][:, : 2 * CHUNK])

        def store(g, rows, queue):
            queue.dma_start(out=out_rows[:, rows, group[g]], in_=o_f32[g][:, rows, :])

        def weave(g, cols):
            nc.vector.tensor_copy(
                out=o_bf[g][:, cols, :].rearrange("p (g i) t -> p g t i", i=4),
                in_=o_f32[g][:, :, cols].rearrange("p t (g i) -> p g t i", i=4),
            )

        def weave_pair(g, u, from_bank):
            src = banks[g][u][:, : 2 * CHUNK].rearrange("p (t c) -> p c t", t=2)
            if not from_bank:
                src = o_f32[g][:, 2 * u : 2 * u + 2, :].rearrange("p t c -> p c t")
            nc.vector.tensor_copy(out=o_bf[g][:, :, 2 * u : 2 * u + 2], in_=src)

        def leave_codes(g, cols):
            dst = slice(starts[g] + cols.start, starts[g] + cols.stop)
            nc.vector.quantize_mx(
                out=o_codes[:, dst].bitcast(FP8X4),
                scales=o_plane[:, dst],
                in_=o_bf[g][:, cols, :].rearrange("p c t -> p (c t)"),
            )

        def store_words(cols, queue):
            queue.dma_start(out=words_dst[:, cols], in_=o_codes[:, cols].bitcast(I32))

        def store_scales(q, queue):
            queue.dma_start(
                out=out_2[0][4 * q : 4 * q + 4, :].bitcast(I32), in_=o_plane[32 * q : 32 * q + 4, :].bitcast(I32)
            )

        by_scalar, by_vector = nc.scalar.copy, nc.vector.tensor_copy
        narrow, wide, upper = slice(0, CHUNK), slice(0, 2 * CHUNK), slice(CHUNK, 2 * CHUNK)
        for c in range(CHUNKS):
            round_z(by_vector if c == 1 else by_scalar, last, chunk[c])
        for g in range(len(widths)):
            second_product(g)
        leave(0, 0, by_scalar)
        store(0, slice(0, 2), nc.sync)
        leave(0, 1, by_scalar)
        store(0, slice(2, 4), nc.sync)
        leave(1, 0, by_vector)
        weave(0, narrow)
        leave(1, 1, by_scalar)
        store(1, slice(0, 4), nc.sync)
        weave(1, narrow)
        leave_codes(0, narrow)
        leave(2, 0, by_scalar)
        leave(2, 1, by_scalar)
        store(2, slice(0, 4), nc.sync)
        weave(2, narrow)
        leave_codes(1, narrow)
        store_words(wide, nc.sync)
        leave(3, 0, by_scalar)
        leave(3, 1, by_scalar)
        store(3, slice(0, 4), nc.scalar)
        weave(3, narrow)
        leave_codes(2, narrow)
        leave_codes(3, narrow)
        store_words(slice(HALF, S), nc.sync)
        store_scales(0, nc.sync)
        store_scales(1, nc.scalar)
        store_scales(2, nc.sync)
        store_scales(3, nc.scalar)
